import numpy as np, ml_dtypes
CORES = [35,38,43,46]
N = 4
import mx_ref
BF = ml_dtypes.bfloat16
def gcols(t, e):
    v = np.concatenate([t.reshape(8, 16, -1, 4), np.zeros((8, 16, 1, 4), BF)], axis=2)
    return np.ascontiguousarray(np.stack([v[g][:, e[g]] for g in range(8)])).reshape(128, -1)
def tile(rs):
    return np.stack(rs, axis=2).reshape(128, -1).astype(BF)
def pick(q, e):
    c = np.concatenate([q[0].reshape(128, -1, 4), np.zeros((128, 1, 4), np.uint8)], axis=1); s = np.concatenate([q[1], np.ones((16, 1), np.uint8)], axis=1)
    return (np.ascontiguousarray(c[:, e].reshape(128, -1)), np.ascontiguousarray(s[:, e]))
def join(*qs):
    return (np.concatenate([q[0] for q in qs], axis=1), np.concatenate([q[1] for q in qs], axis=1))
def put(q, e, v):
    c, s = q[0].reshape(128, -1, 4).copy(), q[1].copy(); c[:, e] = v[0].reshape(128, -1, 4); s[:, e] = v[1]
    return (c.reshape(128, -1), s)
def pk(c, s):
    return (np.ascontiguousarray(c), mx_ref.live(s))
def emit(q):
    return q[0], q[1]
def packed(v, rng):
    q = [mx_ref.quantize(np.ascontiguousarray(v[r])) for r in range(N)]
    return np.stack([a for a, b in q]), np.stack([mx_ref.plane(b, rng) for a, b in q])
def values_of_codes():
    e, c = np.zeros((128, 128, 4), np.float32), np.zeros((128, 2, 4), np.uint8)
    e[np.arange(128), np.arange(128), 0] = 1
    c[:127, :, 0] = np.arange(256).reshape(2, 128).T[:127]
    return mx_ref.matmul(mx_ref.quantize(e.reshape(128, 512).astype(BF)), (c.reshape(128, 8), np.full((16, 2), 127, np.uint8))).T.reshape(-1).astype(np.float64)
CODE_VALUE, SCALE_VALUE = values_of_codes(), 2.0 ** (np.arange(256) - 127.0)
def decode(q):
    return (CODE_VALUE[q[0]].reshape(16, 8, -1, 4) * SCALE_VALUE[q[1]][:, None, :, None] + 0.0).reshape(128, -1).astype(np.float32)
def f(rng, *shape):
    return mx_ref.flush((rng.standard_normal(shape, dtype=np.float32) * np.exp2(rng.integers(-2, 3, shape[:-1] + (1,)))).astype(BF))
def wide(rng, *shape, cols=0):
    v = rng.standard_normal(shape, dtype=np.float32) * np.exp2(rng.integers(-12, 13, shape)).astype(np.float32)
    if cols: v *= np.repeat(np.exp2(rng.integers(-cols, cols + 1, shape[:-2] + (1, shape[-1] // 4))) * (rng.random(shape[:-2] + (1, shape[-1] // 4)) > 0.0625), 4, axis=-1).astype(np.float32)
    return mx_ref.flush(v.astype(BF))
C, H = 384, 192
def order(p):
    return np.argsort(p[::16] + np.float32(0.0), axis=1, kind="stable")
def places(e):
    at = np.full((8, C + H), -1)
    np.put_along_axis(at, e, np.tile(np.arange(C), (8, 1)), axis=1)
    return at
def mean(a, b):
    return ((a.astype(np.float32) + b.astype(np.float32)) * np.float32(0.5)).astype(BF)
def layer(w, q):
    return tile([mx_ref.matmul(pick(w, np.arange(128 * b, 128 * b + 128)), q) * np.float32(0.03125) for b in range(4)])
def big(v, k=1):
    v = v.astype(np.float32) * np.float32(k)
    v[np.abs(v) < np.float32(2.0 ** -16)] = 0
    return v.astype(BF)
def numbers_of(rng):
    return {"x": big(f(rng, N, 128, 4 * C)), "u": np.array(f(rng, N, 128, 512)), "v": np.array(f(rng, N, 128, 512))}
def weights(rng, w):
    c, p = packed(w, rng)
    return {"wc": c, "ws": p}
def still(rng):
    w = np.zeros((N, 128, 4, 128, 4), np.float32)
    i = np.arange(128)
    for b in range(4): w[:, i, b, i, b] = 32
    return weights(rng, w.reshape(N, 128, 2048).astype(BF))
def signs(rng):
    g = rng.permutation(8)
    return ((g[None, :] + np.arange(N)[:, None]) % 4 < 2) * 2.0 - 1.0
def setup_inputs(rng):
    return {**numbers_of(rng), **weights(rng, f(rng, N, 128, 2048))}
def setup_inputs_ties(rng):
    d = numbers_of(rng)
    e = rng.permutation(N)
    x = d["x"].reshape(N, 8, 16, C, 4)
    for r in range(N):
        k = np.zeros(C, int) if r == e[0] else rng.permutation(C) % 3
        a = x[r][:, :8, :3].copy()
        a[:, :, 2] = 0
        x[r][:, :8] = a[:, :, k]
    u = d["u"].reshape(N, 8, 16, 128, 4)
    u[:, :, 8:, ::16] = 0
    w = np.array(f(rng, N, 128, 2048)).reshape(N, 8, 16, 4, 8, 16, 4)
    w[:, :, 8:, :, :, :8] = 0
    return {"x": x.reshape(N, 128, 4 * C), "u": u.reshape(N, 128, 512), "v": d["v"], **weights(rng, w.reshape(N, 128, 2048))}
def setup_inputs_near(rng):
    d = numbers_of(rng)
    x = d["x"].astype(np.float32).reshape(N, 8, 16, C, 4)
    s = (C - 1 - np.arange(C)) // 3
    g = ((s[:, None] >> np.arange(8)) & 1) * np.exp2(np.arange(8) - 23.0)
    sign = signs(rng)
    x[:, :, 0] = 0
    x[:, :, 0, :, 0] = sign[:, :, None]
    x[:, :, 8] = g[:, :4]
    x[:, :, 9] = g[:, 4:]
    x[:, :, 10:] = rng.integers(4, 8, (N, 8, 6, C, 4)) * rng.choice([-1.0, 1.0], (N, 8, 6, C, 4)) * 2.0 ** -20
    u = d["u"].reshape(N, 128, 128, 4)
    small = rng.permutation(N) < N // 2
    one = np.where(small, 0.0, 1.0).astype(np.float32).astype(BF)
    k = np.where(small[:, None], sign * 2.0 ** -30, 1.0).astype(np.float32).astype(BF)
    u[:, :, ::16] = 0
    for i in range(8):
        u[:, 16 * i, 16 * i, 0] = one
        u[:, 16 * i + 8:16 * i + 10, 16 * i] = k[:, i][:, None, None]
    return {"x": x.reshape(N, 128, 4 * C).astype(BF), "u": u.reshape(N, 128, 512), "v": d["v"], **still(rng)}
def setup_inputs_huge(rng):
    d = numbers_of(rng)
    x = 2.0 ** 30 * (0.6 + 0.4 * rng.random((N, 128, C, 4)))
    c = np.stack([rng.permutation(C) % 2 * 2.0 - 1.0 for r in range(N)])
    c[(np.arange(N) + rng.integers(N)) % N < N // 2] = 1
    x *= c[:, None, :, None]
    u = d["u"].reshape(N, 128, 128, 4)
    a = 2.0 ** 30 * (1 - 0.25 * rng.random((N, 128, 8, 4))) * signs(rng)[:, None, :, None]
    u[:, :, ::16] = a.astype(np.float32).astype(BF)
    return {"x": x.astype(np.float32).reshape(N, 128, 4 * C).astype(BF), "u": u.reshape(N, 128, 512), "v": d["v"], **still(rng)}
def setup_inputs_sizes(rng):
    d = setup_inputs(rng)
    d["x"] = big(d["x"], np.exp2(rng.permutation(N) * (16 // N))[:, None, None])
    return d
def setup_inputs_spread(rng):
    d = numbers_of(rng)
    d["x"] = big(wide(rng, N, 128, 4 * C, cols=6))
    w = np.array(f(rng, N, 128, 2048)).reshape(N, 128, 4, 8, 16, 4)
    g = rng.integers(0, 8, N)
    for r in range(N): w[r, :, :, g[r]] = 0
    return {**d, **weights(rng, w.reshape(N, 128, 2048))}
def check_inputs(d):
    b = []
    for k in ("x", "u", "v"):
        a = np.abs(d[k].astype(np.float32))
        if not (np.isfinite(a).all() and ((a == 0) | (a >= 2.0 ** -30) & (a <= 2.0 ** 30)).all()): b.append("a value of " + k)
    if ((d["wc"] == 0x7F) | (d["wc"] == 0xFF)).any(): b.append("a code of wc")
    least, most = [int(mx_ref.quantize(np.full((128, 16), k, np.float32).astype(BF))[1][0, 0]) for k in (2.0 ** -30, 2.0 ** 30)]
    for p in d["ws"]:
        s = mx_ref.live(p)
        if ((s != 1) & ((s < least) | (s > most))).any(): b.append("a scale of ws")
    return b
def reference(x, u, v, wc, ws):
    qu = [mx_ref.quantize(u[r]) for r in range(N)]
    lay = [pk(wc[r], ws[r]) for r in range(N)]
    own, score, lists = [], [], []
    for r in range(N):
        q = mx_ref.quantize(x[r])
        own.append(decode(q).astype(BF))
        score.append(mx_ref.matmul(qu[r], q))
        lists.append([order(score[r])])
    held = [own[r] for r in range(N)]
    for t in range(2):
        pairs = []
        for r in range(N):
            e = lists[r][t]
            pairs.append(mx_ref.quantize(mean(gcols(held[r], e[:, ::2]), gcols(held[r], e[:, 1::2]))))
        for r in range(N):
            q = mx_ref.quantize(layer(lay[r], pairs[(r - 1) % N]))
            held[r] = np.concatenate([own[r], decode(q).astype(BF)], axis=1)
            lists[r].append(order(np.concatenate([score[r], mx_ref.matmul(qu[r], q)], axis=1))[:, :C])
    half = np.tile(np.arange(C) // 2, (8, 1))
    value, used = [], []
    for r in range(N):
        first = layer(lay[r], mx_ref.quantize(gcols(held[r], lists[r][2][:, :H])))
        value.append(np.concatenate([first, np.zeros((128, 4 * (C - H)), BF)], axis=1))
        used.append(np.tile((np.arange(C) < H).astype(np.int64), (8, 1)))
    now = [own[r] for r in range(N)]
    count = [np.zeros((8, C), np.int64) for r in range(N)]
    for t in (2, 1, 0):
        back, flag = [], []
        for r in range(N):
            at = places(lists[r][t])
            is_used = np.take_along_axis(np.concatenate([used[r], np.zeros((8, 1), np.int64)], axis=1), at, axis=1)
            now[r] = mean(now[r], gcols(value[r], at[:, :C]))
            count[r] = count[r] + is_used[:, :C]
            if t > 0:
                back.append(mx_ref.quantize(gcols(value[r], at[:, C:])))
                flag.append(is_used[:, C:])
        if t > 0:
            for r in range(N):
                e = (r + 1) % N
                value[r] = gcols(decode(back[e]).astype(BF), half)
                used[r] = np.take_along_axis(flag[e], half, axis=1)
    y, uc = np.zeros((N, 128, C), np.float32), np.zeros((N, 8, C), np.float32)
    oc, osc = np.zeros((N, 128, 4 * C), np.uint8), np.zeros((N, 16, C), np.uint8)
    for r in range(N):
        q = mx_ref.quantize(now[r])
        y[r] = mx_ref.matmul(mx_ref.quantize(v[r]), q)
        uc[r] = count[r]
        oc[r], osc[r] = emit(q)
    return {"y": y, "uc": uc, "oc": oc, "osc": osc}

@@ -1,0 +1,511 @@
+from concourse.mybir import dt, AluOpType as A, ActivationFunctionType as F
+
+C, H = 384, 192
+X4, U8, BF, F32, I32, U16 = "float8_e4m3fn_x4", "uint8", "bfloat16", "float32", "int32", "uint16"
+NS = (10, 7, 7)
+PW = 208
+BIG = 1.0e29
+
+SCRATCH = {}
+
+
+def _sb(dtype, **kw):
+    for k, n in kw.items():
+        SCRATCH[k] = ("sbuf", [128, n], dtype)
+
+
+_Q = dict(x=C, u=128, ur=128, v=128, w=512, e=512, lx=C, z0=H, z1=H, p1=H, p2=H, lp=H, ee=H, v2=H, lb2=H, b1=H, lb1=H, xx=C)
+for _k, _n in _Q.items():
+    _sb(X4, **{"q_" + _k: _n})
+    _sb(U8, **{"s_" + _k: _n})
+_sb(BF, xb=4 * C, ub=512, vb=512, eb=2048, ones=128, ident=128,
+    m2=C, c16=416, c24=288, iob=PW, mval=H, d0=C, win=2 * 576, ww=2 * 576,
+    tpu=4 * C, tu8=4 * C, heldp=4 * 576, heldo=4 * 576, ztmp=4 * H,
+    z0=4 * H, z1=4 * H, p1=4 * H, p2=4 * H, ee=4 * H, v2=4 * H, b1=4 * H, xx=4 * C,
+    pv=12 * PW, x1=4 * C, x2=4 * C,
+    cmpv=24 * C, scv=24 * H, sig=24 * C, junk=24 * C, eq=C, tie=C, l1=576,
+    fb=224, ft=416, fts=416, mrow=448, mtt=832, o2row=PW, c1row=H, lc1=H,
+    ar=416 * 4, att=800 * 4)
+_sb(F32, io16=C, ior=C, m1=C, cols=8, jj=32, i16=32, s192=48, cb=48, tmp=160,
+    srow=C, prow=2 * H, msk=C, hh=C + 2 * H, a1=48, a2=48, tb=48, tb2=48, tb3=48, dd=48, rk=48, l0w=448, l0t=832,
+    ss=416, sst=816, ssw=32, spl=288, g1=128, cf=128, ucr=2 * C, yb=C)
+_sb(I32, pi=8, qi=32, hi=96)
+_sb(U16, uo=8, ko=52, rku=48, e0=32, o1=32, lst=112, le0=24, lo1=24, loff2=12, xo=128)
+SCRATCH["ps"] = ("psum", [128, 4096], F32)
+
+_DMA = ["x0", "x1", "u", "wc", "ws", "v", "oc0", "oc1", "os0", "os1", "osg", "y0", "y1", "uc"]
+_REM = ["qx", "sx", "e0", "qp", "sp", "o1", "off2", "qv2", "sv2", "c1", "qb1", "sb1"]
+SEMAPHORES = ["cV", "cS", "cT", "cG", "sent"] + ["d_" + k for k in _DMA] + ["r_" + k for k in _REM]
+
+
+def rank_program(g, core, T, topo):
+    rank = T.rank_of(core)
+    if rank is None:
+        return
+    N = len(T.cores)
+    nxt, prv = T.cores[(rank + 1) % N], T.cores[(rank - 1) % N]
+    Q = {"V": g.vector, "S": g.scalar, "T": g.tensor, "G": g, "Y": g.sync}
+    cnt, seen, wr, rd = {}, {q: {} for q in Q}, {}, {}
+
+    def need(q, r, w):
+        deps = {}
+        for k in list(r) + list(w):
+            if k in wr:
+                deps[wr[k][0]] = max(deps.get(wr[k][0], 0), wr[k][1])
+        for k in w:
+            for s, n in rd.get(k, {}).items():
+                deps[s] = max(deps.get(s, 0), n)
+        for k in r:
+            if k.startswith("ps"):
+                for s, n in rd.get(k, {}).items():
+                    if s != "c" + q:
+                        deps[s] = max(deps.get(s, 0), n)
+        for s, n in deps.items():
+            if seen[q].get(s, 0) < n:
+                Q[q].wait_ge(T.sem[s], n)
+                seen[q][s] = n
+
+    def mark(s, n, r, w):
+        for k in r:
+            rd.setdefault(k, {})[s] = n
+        for k in w:
+            wr[k] = (s, n)
+            rd[k] = {}
+
+    def op(q, fn, r, w):
+        need(q, r, w)
+        s = "c" + q
+        cnt[s] = cnt.get(s, 0) + 1
+        fn().then_inc(T.sem[s], 1)
+        mark(s, cnt[s], r, w)
+
+    def dma(q, name, out, in_, r, w, **kw):
+        need(q, r, w)
+        s = "d_" + name
+        cnt[s] = cnt.get(s, 0) + 16
+        Q[q].dma_start(out, in_, **kw).then_inc(T.sem[s], 16)
+        mark(s, cnt[s], r, w)
+
+    def send(name, dst, out, in_, r, land):
+        need("G", r, [])
+        rid, pid, _ = topo.addr(dst)
+        g.remote_dma(out, in_, T.sem["r_" + name], T.sem.sent, pid, rid, topo.mask(core, dst))
+        cnt["sent"] = cnt.get("sent", 0) + len(topo.engines(core, dst))
+        src = prv if dst == nxt else nxt
+        cnt["r_" + name] = len(topo.engines(src, core))
+        wr[land] = ("r_" + name, cnt["r_" + name])
+
+    def sendq(name, dst, a, b):
+        send("q" + name, dst, T["q_" + b][:].bitcast(dt.uint8), T["q_" + a][:].bitcast(dt.uint8), ["q_" + a], "q_" + b)
+        send("s" + name, dst, T["s_" + b][:], T["s_" + a][:], ["q_" + a], "s_" + b)
+
+    V, S, IO = g.vector, g.scalar, T.ior
+    fl = dict(allow_small_or_imprecise_dtypes=True)
+
+    def ts(out, in0, s1, op0, s2, op1, r, w):
+        if op1 is None:
+            op("V", lambda: V.tensor_scalar(out, in0, s1, None, op0), r, w)
+        else:
+            op("V", lambda: V.tensor_scalar(out, in0, s1, s2, op0, op1), r, w)
+
+    def tt(out, in0, in1, o, r, w):
+        op("V", lambda: V.tensor_tensor(out, in0, in1, o), r, w)
+
+    def cp(out, in_, r, w):
+        op("V", lambda: V.tensor_copy(out, in_), r, w)
+
+    def ms(out, c, w):
+        op("V", lambda: V.memset(out, c), [], w)
+
+    def gfill(out, n, c, w):
+        op("G", lambda: g.iota(out, [[0, n]], c, 0, **fl), [], w)
+
+    def scan(out, d0, d1, o0, r, w):
+        op("V", lambda: V.tensor_tensor_scan(out, d0, d1, 0.0, o0, A.add), r, w)
+
+    def tr(out, in_, r, w):
+        op("V", lambda: V.transpose(out, in_), r, w)
+
+    def act(out, in_, f, r, w, **kw):
+        op("S", lambda: S.activation(out, in_, f, **kw), r, w)
+
+    def quant(name, src, a=0, b=None, key=None, rk=None):
+        b = _Q[name] if b is None else b
+        op("V", lambda: V.quantize_mx(T["q_" + name][:, a:b], T["s_" + name][:, a:b], T[src][:, 4 * a:4 * b]),
+           rk or [src + str(i) for i in range(4)], [key or "q_" + name])
+
+    def mm(bank, st, c0, mv, a, b, r):
+        op("T", lambda: g.tensor.matmul_mx(T.ps[:, 512 * bank:512 * bank + b - a], T["q_" + st][:, c0:c0 + 128], T["s_" + st][:, c0:c0 + 128],
+                                           T["q_" + mv][:, a:b], T["s_" + mv][:, a:b], True, True), r, ["ps%d" % bank])
+
+    def ps(bank, n):
+        return T.ps[:, 512 * bank:512 * bank + n]
+
+    def four(st, mv, banks, n):
+        for b in range(4):
+            mm(banks[b], st, 128 * b, mv, 0, n, ["q_" + st, "s_" + st, "q_" + mv, "s_" + mv])
+
+    def evac(q, out, bank, n, scale, w):
+        if q == "V":
+            ts(out, ps(bank, n), scale, A.mult, None, None, ["ps%d" % bank], w)
+        else:
+            act(out, ps(bank, n), F.Identity, ["ps%d" % bank], w, scale=scale)
+
+    def to_tile(name, banks, scale):
+        for b, q in ((0, "V"), (1, "S"), (2, "V"), (3, "S")):
+            evac(q, T[name][:, b:4 * H:4], banks[b], H, scale, [name + str(b)])
+
+    KC, ODD, P208, P400, ODD1, K1024, EVEN = [T.cols[:, i:i + 1] for i in range(7)]
+    SELN, SELB, SELE, REP, SPLO = T.ko[:, 0:2], T.ko[:, 2:4], (T.ko[:, 4:6], T.ko[:, 6:8]), T.ko[:, 14:32], T.ko[:, 32:50]
+    SEL12 = [T.ko[:, 8 + 2 * i:9 + 2 * i] for i in range(3)]
+    O2, P1H, A0H, CU, OFF2 = T.lst[:, 0:12], T.lst[:, 36:48], T.lst[:, 48:72], T.lst[:, 72:96], T.lst[:, 96:108]
+    tm = lambda a, n: T.tmp[:, a:a + n]
+    A4, B4 = (2, 3, 4, 5), (6, 7, 6, 7)
+    OFS = (0, 24, 36)
+
+    dma("S", "u", T.ub[:], T.u[:], [], ["ub"])
+    dma("Y", "x0", T.xb[:, 0:768], T.x[:, 0:768], [], ["xb0"])
+    dma("Y", "x1", T.xb[:, 768:1536], T.x[:, 768:1536], [], ["xb1"])
+    dma("Y", "wc", T.q_w[:].bitcast(dt.uint8), T.wc[:], [], ["q_w"])
+    dma("Y", "ws", T.s_w[:], T.ws[:], [], ["s_w"])
+    dma("Y", "v", T.vb[:], T.v[:], [], ["vb"])
+    op("G", lambda: g.iota(T.pi[:, 0:1], [[0, 1]], 0, 1), [], ["pi0"])
+    op("G", lambda: g.iota(T.qi[:, 0:8], [[16, 8]], 0, 0), [], ["qi"])
+    ms(T.ones[:], 1.0, ["ones"])
+    op("G", lambda: g.iota(T.io16[:], [[0, 24], [1, 16]], 0, 0, **fl), [], ["io16"])
+    op("G", lambda: g.affine_select(T.ident[:], T.ones[:], [[-1, 128]], A.is_equal, 0.0, 0, 1), ["ones"], ["ident"])
+    op("G", lambda: g.iota(T.i16[:], [[16, 32]], 0, 0, **fl), [], ["i16"])
+    op("G", lambda: g.iota(IO[:], [[1, C]], 0, 0, **fl), [], ["io"])
+    ms(T.eb[:], 0.0, ["eb"])
+    ts(T.pi[:, 1:2], T.pi[:, 0:1], 4, A.arith_shift_right, None, None, ["pi0"], ["pi1"])
+    ts(T.pi[:, 4:5], T.pi[:, 0:1], 15, A.bitwise_and, None, None, ["pi0"], ["pi4"])
+    ts(T.pi[:, 5:6], T.pi[:, 0:1], 1, A.bitwise_and, None, None, ["pi0"], ["pi5"])
+    cp(T.uo[:], T.qi[:, 0:8], ["qi"], ["uo"])
+    ms(T.c16[:], 1.0, ["c16"])
+    tt(T.pi[:, 2:3], T.pi[:, 0:1], T.pi[:, 1:2], A.add, ["pi0", "pi1"], ["pi2"])
+    cp(T.cols[:, 0:2], T.pi[:, 4:6], ["pi4", "pi5"], ["col0"])
+    ms(T.c16[:, 0:416:16], 0.0, ["c16"])
+    ts(T.pi[:, 3:4], T.pi[:, 2:3], 1, A.bitwise_and, None, None, ["pi2"], ["pi3"])
+    ts(T.m1[:], T.io16[:], KC, A.is_equal, None, None, ["io16", "col0"], ["m1"])
+    ts(T.m2[:], T.io16[:], KC, A.is_gt, None, None, ["io16", "col0"], ["m2"])
+    for b in range(4):
+        act(T.eb[:, 512 * b + b:512 * b + 512:4], T.ident[:], F.Copy, ["ident", "eb"], ["eb%d" % b])
+    quant("u", "ub", rk=["ub"])
+    ts(P208, T.pi[:, 3:4], 208.0, A.mult, None, None, ["pi3"], ["col2"])
+    op("V", lambda: V.tensor_copy(T.q_ur[:].bitcast(dt.uint32), T.q_u[:].bitcast(dt.uint32).indirect(T.uo[:])), ["q_u", "uo"], ["q_ur"])
+    act(T.s_ur[:], T.s_u[:].indirect(T.uo[:]), F.Copy, ["q_u", "uo"], ["s_ur"])
+    quant("x", "xb", 0, H, "q_x0", ["xb0"])
+    quant("e", "eb", rk=["eb0", "eb1", "eb2", "eb3"])
+    quant("x", "xb", H, C, "q_x", ["xb1"])
+    mm(0, "ur", 0, "x", 0, C, ["q_ur", "s_ur", "q_x0", "q_x"])
+    mm(1, "ur", 0, "x", 0, C, ["q_ur", "s_ur", "q_x0", "q_x"])
+    sendq("x", nxt, "x", "lx")
+    ts(ODD1, ODD, -1.0, A.add, None, None, ["col0"], ["col4"])
+    ts(K1024, ODD, 1024.0, A.mult, None, None, ["col0"], ["col5"])
+    ts(EVEN, ODD, -1.0, A.mult, 1.0, A.add, ["col0"], ["col6"])
+    ts(T.jj[:], T.i16[:], KC, A.add, None, None, ["i16", "col0"], ["jj"])
+    for t, n in ((0, 24), (1, 12), (2, 12)):
+        o, ns = OFS[t], NS[t]
+        act(T.cb[:, o:o + ns], T.i16[:, 1:ns + 1], F.Copy, ["i16"], ["cb%d" % t])
+        act(T.cb[:, o + ns:o + n], T.i16[:, 0:n - ns], F.Identity, ["i16"], ["cb%db" % t], scale=0.0, bias=float(8 * n))
+    act(T.iob[:], IO[:, 0:PW], F.Copy, ["io"], ["iob"])
+    gfill(T.l0w[:, 0:32], 32, 0, ["l0p"])
+    gfill(T.l0w[:, 416:448], 32, 0, ["l0p2"])
+    gfill(T.ss[:, 0:16], 16, 0, ["ssp"])
+    gfill(T.ss[:, 400:416], 16, 0, ["ssp2"])
+    gfill(T.c24[:], 288, 1, ["c24"])
+    gfill(T.c24[:, 0:288:24], 12, 0, ["c24"])
+    gfill(T.fb[:], 224, 0, ["fb"])
+    gfill(T.mrow[:], 448, 0, ["mrow"])
+    gfill(T.ww[:], 2 * 576, 192, ["w1", "w2"])
+    gfill(T.ar[:], 4 * 416, 0, ["arp"])
+    gfill(T.o2row[:, H:PW], 16, 192, ["o2p"])
+    gfill(T.pv[:, H:12 * PW:PW], 12, 0, ["pvz"])
+
+    def sacc(m, n, o, tg):
+        e = 16 * (m + 1)
+        act(T.junk[:, C * m:C * m + e], T.sig[:, C * m:C * m + e], F.Relu, ["sig%d" % m], ["jk%d" % m, "a1_%s%d" % (tg, m)],
+            scale=-1.0, accum_out=T.a1[:, o + m:o + m + 1])
+        act(T.junk[:, C * m + e:C * m + n], T.sig[:, C * m + e:C * m + n], F.Relu, ["sig%d" % m], ["jl%d" % m, "a2_%s%d" % (tg, m)],
+            accum_out=T.a2[:, o + m:o + m + 1])
+
+    def ranking(t, n, row, hb, chain):
+        nm, tg, ns, o = n // 16, str(t), NS[t], OFS[t]
+        hh = T.hh[:, hb:hb + n]
+        act(row, ps(1, n), F.Copy, ["ps1"], ["row" + tg])
+        tt(T.msk[:, 0:n], ps(0, n), T.m1[:, 0:n], A.mult, ["ps0", "m1"], ["msk"])
+        scan(hh, T.c16[:, 0:n], T.msk[:, 0:n], A.mult, ["c16", "msk"], ["hh" + tg])
+        own = lambda m: T.hh[:, hb + 16 * m + 15:hb + 16 * m + 16]
+        for m in range(ns):
+            act(T.sig[:, C * m:C * m + n], row, F.Sign, ["row" + tg, "hh" + tg], ["sig%d" % m], scale=-1.0, bias=own(m))
+            if m > 0:
+                sacc(m - 1, n, o, tg)
+        sacc(ns - 1, n, o, tg)
+        fill = [lambda: tt(T.eq[:, 0:n], ps(0, n), hh, A.is_equal, ["ps0", "hh" + tg], ["eq"]),
+                lambda: scan(T.tie[:, 0:n], T.m2[:, 0:n], T.eq[:, 0:n], A.mult, ["m2", "eq"], ["tie"]),
+                lambda: tt(T.tb[:, o:o + nm], T.cb[:, o:o + nm], T.tie[:, 15:n:16], A.subtract, ["cb" + tg, "cb%sb" % tg, "tie"], ["tb" + tg])]
+
+        def vrow(m):
+            e = 16 * (m + 1)
+            ts(T.cmpv[:, C * m:C * m + e], T.ps[:, 0:e], own(m), A.is_le, -0.5, A.add, ["ps0", "hh" + tg], ["cv%d" % m])
+            if e < n:
+                ts(T.cmpv[:, C * m + e:C * m + n], T.ps[:, e:n], own(m), A.is_lt, -0.5, A.add, ["ps0", "hh" + tg], ["cw%d" % m])
+
+        def vsum(m):
+            h = n // 2
+            scan(T.scv[:, h * m:h * m + h], T.cmpv[:, C * m:C * m + h], T.cmpv[:, C * m + h:C * m + n], A.add, ["cv%d" % m, "cw%d" % m], ["sc%d" % m])
+
+        rows = []
+        for m in range(ns, nm):
+            rows.append(lambda m=m: (vrow(m), vsum(m - 1) if m > ns else None))
+        rows.append(lambda: vsum(nm - 1))
+        if chain:
+            order, rest = [], fill + rows
+            for c in chain:
+                order.append(c)
+                if rest:
+                    order.append(rest.pop(0))
+            order += rest
+        else:
+            order = [fill[0], rows[0], fill[1], rows[1], fill[2]] + rows[2:]
+        for f in order:
+            f()
+
+    def places(t, n, base, bkey):
+        nm, tg, h, ns, o = n // 16, str(t), n // 2, NS[t], OFS[t]
+        tt(T.dd[:, o:o + ns], T.a2[:, o:o + ns], T.a1[:, o:o + ns], A.subtract,
+           ["a%d_%s%d" % (i, tg, m) for m in range(ns) for i in (1, 2)], ["dd" + tg])
+        tt(T.rk[:, o + ns:o + nm], T.scv[:, h * ns + h - 1:h * nm:h], base[:, o + ns:o + nm], A.add,
+           ["sc%d" % m for m in range(ns, nm)] + [bkey], ["rkv" + tg])
+        tt(T.rk[:, o:o + ns], T.dd[:, o:o + ns], base[:, o:o + ns], A.add, ["dd" + tg, bkey], ["rks" + tg])
+        cp(T.rku[:, o:o + nm], T.rk[:, o:o + nm], ["rkv" + tg, "rks" + tg], ["rku" + tg])
+
+    def turn_eo(dst, src, r, w):
+        for o in (0, 1):
+            tr(dst[:, 416 * o:416 * o + H], src[:, 32 + o:32 + o + C - 1:2], r, [w + "a%d" % o])
+            tr(dst[:, 416 * o + H:416 * o + 416], src[:, o:o + 447:2], r, [w + "b%d" % o])
+        return [w + x for x in ("a0", "b0", "a1", "b1")]
+
+    def turn(dst, d0, src, s0, n, r, w):
+        tr(dst[:, d0:d0 + n], src[:, s0 + 16:s0 + 16 + n], r, [w + "a0"])
+        tr(dst[:, d0 + n:d0 + 2 * n + 32], src[:, s0:s0 + n + 32], r, [w + "b0"])
+        return [w + "a0", w + "b0"]
+
+    def wrap_s(i, win, offs, r):
+        act(T.ar[:, 416 * i + 16:416 * i + 400], win.indirect(offs), F.Copy, r + ["arp"], ["ar%d" % i])
+
+    def wrap_v(i):
+        kk = turn(T.att, 800 * i, T.ar, 416 * i, C, ["ar%d" % i], "att%d" % i)
+        cp(T.xo[:, 32 * i:32 * i + 32], T.att[:, 800 * i:800 * i + 800].indirect(SELN), kk + ["seln"], ["xo%d" % i])
+
+    def init_win(t):
+        a = 576 * (t - 1)
+        act(T.win[:, a:a + C], IO[:], F.Identity, ["io", "col5"], ["win%d" % t], scale=0.0, bias=K1024)
+        act(T.win[:, a + C:a + 576], IO[:, 0:H], F.Identity, ["io", "col5"], ["win%db" % t], scale=0.0, bias=K1024)
+
+    def sort_own(b):
+        for o in range(2):
+            act(T.heldo[:, 576 * b + H + o:576 * b + 576:2], T.tu8[:, C * b:C * b + C].indirect(T.e0[:, 12 * o:12 * o + 12]), F.Copy,
+                ["tu8%d" % b, "e0"], ["ho%d%d" % (b, o)])
+
+    ranking(0, C, T.srow[:], 0, None)
+    ts(tm(0, 2), T.jj[:, 0:2], 12.0, A.is_ge, 224.0, A.mult, ["jj"], ["t0"])
+    ts(tm(2, 2), T.jj[:, 0:2], 16.0, A.mult, P208, A.add, ["jj", "col2"], ["t2"])
+    tt(tm(4, 2), tm(0, 2), tm(2, 2), A.add, ["t0", "t2"], ["t4"])
+    places(0, C, T.tb, "tb0")
+    four("e", "lx", A4, C)
+    cp(T.l0w[:, 32:416].indirect(T.rku[:, 0:24]), IO[:], ["rku0", "io"], ["l0w"])
+    ts(SELE[0], tm(4, 2), 831.0, A.min, None, None, ["t4"], ["sele0"])
+    for b in range(4):
+        evac("S", T.tpu[:, C * b:C * b + C], A4[b], C, 0.5, ["tpu%d" % b])
+    k = turn_eo(T.l0t, T.l0w, ["l0w", "l0p", "l0p2"], "l0t")
+    cp(T.e0[:], T.l0t[:].indirect(SELE[0]), k + ["sele0"], ["e0"])
+    send("e0", nxt, T.le0[:], T.e0[:, 0:24], ["e0"], "le0")
+    for b in range(4):
+        mm(B4[b], "e", 128 * b, "x", 0, C, ["q_e", "q_x"])
+        if b < 3:
+            evac("S", T.tu8[:, C * b:C * b + C], B4[b], C, 0.125, ["tu8%d" % b])
+
+    cp(T.ss[:, 16:400:2], T.srow[:].indirect(T.e0[:, 0:12]), ["row0", "e0"], ["ss0"])
+    act(T.ss[:, 17:400:2], T.srow[:].indirect(T.e0[:, 12:24]), F.Copy, ["row0", "e0"], ["ss1"])
+    ts(P400, T.pi[:, 3:4], 400.0, A.mult, None, None, ["pi3"], ["col3"])
+    ts(tm(8, 2), T.jj[:, 0:2], 24.0, A.is_ge, 1000.0, A.mult, ["jj"], ["t8"])
+    ts(tm(16, 18), T.jj[:, 0:18], -11.5, A.add, 1.0 / 24.0, A.mult, ["jj"], ["t16"])
+    ts(tm(6, 2), T.jj[:, 0:2], 16.0, A.mult, P400, A.add, ["jj", "col3"], ["t6"])
+    cp(T.qi[:, 8:26], tm(16, 18), ["t16"], ["qi8"])
+    ms(T.sst[:, 800:816], BIG, ["sstp"])
+    tt(tm(10, 2), tm(6, 2), tm(8, 2), A.add, ["t6", "t8"], ["t10"])
+    ts(tm(40, 18), T.qi[:, 8:26], -24.0, A.mult, None, None, ["qi8"], ["t40"])
+    k = turn(T.sst, 0, T.ss, 0, C, ["ssp", "ssp2", "ss0", "ss1"], "sst")
+    tt(tm(60, 18), tm(40, 18), T.jj[:, 0:18], A.add, ["t40", "jj"], ["t60"])
+    ts(SELB, tm(10, 2), 800.0, A.min, None, None, ["t10"], ["selb"])
+    ts(SPLO, tm(60, 18), 16.0, A.mult, 15.0, A.add, ["t60"], ["splo"])
+    ts(REP, T.qi[:, 8:26], 16.0, A.mult, 15.0, A.add, ["qi8"], ["rep"])
+    cp(T.ssw[:], T.sst[:].indirect(SELB), k + ["sstp", "selb"], ["ssw"])
+    ts(SELE[1], tm(4, 2), 1.0, A.add, 831.0, A.min, ["t4"], ["sele1"])
+    for i, r0 in enumerate((0.0, 1.0, 15.0)):
+        ts(SEL12[i], tm(2, 1), r0, A.add, 415.0, A.min, ["t2"], ["sel12%d" % i])
+    evac("S", T.tu8[:, C * 3:C * 4], B4[3], C, 0.125, ["tu83"])
+    init_win(1)
+    act(T.d0[:], IO[:], F.Identity, ["io", "col6"], ["d0"], scale=0.0, bias=EVEN)
+    act(T.mval[:], IO[:, 0:H], F.Identity, ["io", "col0", "col4"], ["mval"], scale=ODD, bias=ODD1)
+
+    def zmake(t, win, stride, wkeys, lst, lkey, tmp, gaps, sgap):
+        z = "z%d" % t
+        for b in range(4):
+            w = win[:, stride * b:stride * b + stride]
+            act(tmp(b), w.indirect(lst[:, 12:24]), F.Copy, wkeys(b) + [lkey], ["zt%d%d" % (t, b)])
+            tt(T[z][:, b:4 * H:4], w.indirect(lst[:, 0:12]), tmp(b), A.add, wkeys(b) + [lkey, "zt%d%d" % (t, b)], [z + str(b)])
+        quant(z, z)
+        sgap()
+        four("w", z, A4, H)
+        gaps[0]()
+        p = "p%d" % (t + 1)
+        to_tile(p, A4, 0.03125)
+        quant(p, p)
+        mm(0, "ur", 0, p, 0, H, ["q_" + p])
+        mm(1, "ur", 0, p, 0, H, ["q_" + p])
+        gaps[1]()
+
+    def merge(t):
+        tg, o, hb = str(t), OFS[t], C + H * (t - 1)
+        row, bo = T.prow[:, H * (t - 1):H * t], T.lst[:, 12 * t:12 * t + 12]
+        ends = T.l1[:, 288 + 23:576:24]
+        chain = [
+            lambda: tt(T.l1[:, 0:288], T.hh[:, hb:hb + H].indirect(REP), T.spl[:], A.is_ge, ["hh" + tg, "rep", "spl"], ["l1"]),
+            lambda: scan(T.l1[:, 288:576], T.c24[:], T.l1[:, 0:288], A.mult, ["c24", "l1"], ["l1s"]),
+            lambda: cp(bo, ends, ["l1s"], ["bo" + tg]),
+            lambda: tt(T.fb[:, 16:208], T.ssw[:].indirect(bo), row, A.is_le, ["ssw", "bo" + tg, "row" + tg], ["fb"]),
+            lambda: (turn(T.ft, 0, T.fb, 0, H, ["fb"], "ft"),
+                     ts(T.tb2[:, o:o + 12], ends, 16.0, A.mult, None, None, ["l1s"], ["tb2" + tg])),
+            lambda: (scan(T.fts[:], T.c16[:], T.ft[:], A.mult, ["c16", "fta0", "ftb0"], ["fts"]),
+                     tt(T.tb3[:, o:o + 12], T.tb2[:, o:o + 12], T.tb[:, o:o + 12], A.add, ["tb2" + tg, "tb" + tg], ["tb3" + tg])),
+            lambda: cp(T.g1[:, 0:16], T.fts[:].indirect(SEL12[2]), ["fts", "sel122"], ["g1"]),
+            lambda: tt(T.tb2[:, o:o + 12], T.g1[:, 0:12], T.tb3[:, o:o + 12], A.add, ["g1", "tb3" + tg], ["tb2" + tg]),
+        ]
+        ranking(t, H, row, hb, chain)
+        places(t, H, T.tb2, "tb2" + tg)
+        if t == 2:
+            ts(OFF2, T.rk[:, 36:48], 192.0, A.min, None, None, ["rkv2", "rks2"], ["off2"])
+            send("off2", prv, T.loff2[:], OFF2, ["off2"], "loff2")
+        cp(T.win[:, 576 * (t - 1):576 * t].indirect(T.rku[:, o:o + 12]), T.mval[:], ["rku" + tg, "mval"], ["win" + tg, "win%sb" % tg])
+
+    zmake(0, T.tpu, C, lambda b: ["tpu%d" % b], T.le0, "le0", lambda b: T.heldp[:, 576 * b + H + 1:576 * b + 576:2],
+          [lambda: (ts(tm(80, 32), T.jj[:], 192.0, A.is_ge, -383.0, A.mult, ["jj"], ["t80"]),
+                    ts(tm(112, 32), T.jj[:], 2.0, A.mult, 192.0, A.add, ["jj"], ["t112"])),
+           lambda: (tt(T.s192[:, 0:32], tm(80, 32), tm(112, 32), A.add, ["t80", "t112"], ["s192e"]),
+                    ts(SELN, tm(6, 2), 799.0, A.min, None, None, ["t6"], ["seln"]))],
+          lambda: act(T.spl[:], T.ss[:, 16:400].indirect(SPLO), F.Copy, ["ss0", "ss1", "splo"], ["spl"]))
+    sendq("p", nxt, "p1", "lp")
+    merge(1)
+    four("e", "lp", A4, H)
+    scan(T.mrow[:, 32:416], T.d0[:], T.win[:, 0:C], A.mult, ["d0", "win1"], ["mrow"])
+    for b in range(4):
+        act(T.heldp[:, 576 * b + H:576 * b + 576:2], T.tpu[:, C * b:C * b + C].indirect(T.le0[:, 0:12]), F.Copy,
+            ["tpu%d" % b, "le0"], ["hpe%d" % b])
+    k = turn_eo(T.mtt, T.mrow, ["mrow"], "mtt")
+    tt(T.g1[:, 32:64], T.mtt[:].indirect(SELE[0]), T.s192[:, 0:32], A.add, k + ["sele0", "s192e"], ["g1b"])
+    tt(T.g1[:, 64:96], T.mtt[:].indirect(SELE[1]), T.g1[:, 32:64], A.min, k + ["sele1", "g1b"], ["g2b"])
+    cp(T.o1[:, 0:24], T.g1[:, 64:88], ["g2b"], ["o1"])
+    send("o1", nxt, T.lo1[:], T.o1[:, 0:24], ["o1"], "lo1")
+
+    for o in range(2):
+        cp(T.ww[:, 0:576].indirect(T.o1[:, 12 * o:12 * o + 12]), T.iob[:, 0:H], ["o1", "iob"], ["w1"])
+    for b in range(4):
+        evac("S", T.heldp[:, 576 * b:576 * b + H], A4[b], H, 0.5, ["hpp%d" % b])
+    sort_own(0)
+    sort_own(1)
+    wrap_s(3, T.ww[:, H:576], T.rku[:, 0:24], ["w1", "rku0"])
+    init_win(2)
+    cp(T.hi[:, 0:36], T.rk[:, 0:36], ["rkv0", "rks0", "rkv1", "rks1"], ["hi"])
+    quant("v", "vb", rk=["vb"])
+    ts(T.hi[:, 48:84], T.hi[:, 0:36], 1, A.arith_shift_right, None, None, ["hi"], ["hi2"])
+    wrap_v(3)
+    zmake(1, T.heldp, 576, lambda b: ["zt0%d" % b, "hpe%d" % b, "hpp%d" % b], T.lo1, "lo1", lambda b: T.ztmp[:, H * b:H * b + H],
+          [lambda: (ts(P1H, T.hi[:, 72:84], 192.0, A.min, None, None, ["hi2"], ["p1h"]),
+                    cp(A0H, T.hi[:, 48:72], ["hi2"], ["a0h"])),
+           lambda: ts(T.s192[:, 32:48], T.jj[:, 0:16], 192.0, A.add, None, None, ["jj"], ["s192n"])],
+          lambda: sort_own(2))
+    four("e", "p2", A4, H)
+    merge(2)
+    scan(T.mrow[:, 32:32 + H], T.d0[:, 0:H], T.win[:, 576:576 + H], A.mult, ["d0", "win2"], ["mrow"])
+    for b in range(4):
+        evac("S", T.heldo[:, 576 * b:576 * b + H], A4[b], H, 0.125, ["hop%d" % b])
+    sort_own(3)
+    k = turn(T.mtt, 0, T.mrow, 16, H, ["mrow"], "mtt")
+    tt(T.g1[:, 16:32], T.mtt[:, 0:416].indirect(SEL12[0]), T.s192[:, 32:48], A.add, k + ["sel120", "s192n"], ["g1c"])
+    tt(T.g1[:, 96:112], T.mtt[:, 0:416].indirect(SEL12[1]), T.g1[:, 16:32], A.min, k + ["sel121", "g1c"], ["g2"])
+    cp(O2, T.g1[:, 96:108], ["g2"], ["o2"])
+    for b in (0, 2, 1, 3):
+        w, r = T.heldo[:, 576 * b:576 * b + 576].indirect(O2), ["hop%d" % b, "ho%d0" % b, "ho%d1" % b, "o2"]
+        if b < 2:
+            ts(T.ee[:, b:4 * H:4], w, 8.0, A.mult, None, None, r, ["ee%d" % b])
+        else:
+            act(T.ee[:, b:4 * H:4], w, F.Identity, r, ["ee%d" % b], scale=8.0)
+    quant("ee", "ee")
+    four("w", "ee", A4, H)
+    to_tile("v2", A4, 0.03125)
+    quant("v2", "v2")
+    sendq("v2", prv, "v2", "lb2")
+
+    def leaves(out, i, prev, b, a, e, r, w):
+        c0 = PW * (4 * i + b)
+        tt(out, T.pv[:, c0:c0 + PW].indirect(T.xo[:, 32 * i + a // 16:32 * i + e // 16]), T[prev][:, C * b + a:C * b + e], A.add,
+           r + ["xo%d" % i, "pvz", "pv%d%d" % (i, b)], w)
+
+    def planes(i, b, scale):
+        c0 = PW * (4 * i + b)
+        evac("S", T.pv[:, c0:c0 + H], A4[b], H, scale, ["pv%d%d" % (i, b)])
+
+    act(T.o2row[:, 0:H], T.iob[:].indirect(T.loff2[:]), F.Copy, ["iob", "loff2"], ["o2row"])
+    wrap_s(1, T.o2row[:], T.xo[:, 96:120], ["o2row", "o2p", "xo3"])
+    cp(T.ww[:, 576:1152].indirect(O2), T.iob[:, 0:H], ["o2", "iob"], ["w2"])
+    wrap_s(0, T.ww[:, 576 + H:1152], T.rku[:, 0:24], ["w2", "rku0"])
+    planes(0, 0, 0.03125 / 8)
+    act(T.c1row[:], T.o2row[:].indirect(P1H), F.Copy, ["o2row", "o2p", "p1h"], ["c1row"])
+    send("c1", prv, T.lc1[:], T.c1row[:], ["c1row"], "lc1")
+    for b in range(1, 4):
+        planes(0, b, 0.03125 / 8)
+    wrap_v(1)
+    wrap_v(0)
+    for b in range(3):
+        leaves(T.x1[:, C * b:C * b + C], 0, "tu8", b, 0, C, ["tu8%d" % b], ["x1%d" % b])
+        if b == 0:
+            ts(T.cf[:, 0:64], T.xo[:, 0:64], 192.0, A.is_lt, None, None, ["xo0", "xo1"], ["cf0"])
+        elif b == 1:
+            tt(T.cf[:, 96:120], T.cf[:, 0:24], T.cf[:, 32:56], A.add, ["cf0"], ["cf3"])
+        else:
+            cp(CU, T.cf[:, 96:120], ["cf3"], ["cu"])
+    four("e", "lb2", A4, H)
+    to_tile("b1", A4, 1.0)
+    quant("b1", "b1")
+    sendq("b1", prv, "b1", "lb1")
+
+    for b in range(4):
+        planes(1, b, 0.25)
+    wrap_s(2, T.lc1[:], A0H, ["lc1", "a0h"])
+    act(T.ucr[:, 0:C], IO[:, 0:16].indirect(CU), F.Copy, ["io", "cu"], ["ucr"])
+    dma("Y", "uc", T.uc[:], T.ucr[0:128:16, 0:C], ["ucr"], ["uc"])
+    act(T.ucr[:, C:2 * C], T.ar[:, 832 + 16:832 + 400], F.Sign, ["ar2"], ["ucr2"], scale=-1.0, bias=192.0)
+    dma("G", "osg", T.uc[:], T.ucr[0:128:16, C:2 * C], ["ucr2", "uc"], [], accum_op=A.add)
+    leaves(T.x1[:, C * 3:C * 4], 0, "tu8", 3, 0, C, ["tu83"], ["x13"])
+    for b in range(4):
+        leaves(T.x2[:, C * b:C * b + C], 1, "x1", b, 0, C, ["x1%d" % b], ["x2%d" % b])
+        if b == 1:
+            wrap_v(2)
+    four("e", "lb1", A4, H)
+    for b in range(4):
+        planes(2, b, 0.5)
+    for hf, (a, e) in enumerate(((0, 256), (256, C))):
+        for b in range(4):
+            leaves(T.xx[:, 4 * a + b:4 * e:4], 2, "x2", b, a, e, ["x2%d" % b], ["xx%d%d" % (hf, b)])
+        quant("xx", "xx", a, e, "q_xx%d" % hf, ["xx%d%d" % (hf, b) for b in range(4)])
+        mm(hf, "v", 0, "xx", a, e, ["q_v", "q_xx%d" % hf])
+        dma("Y", "oc%d" % hf, T.oc[:, 4 * a:4 * e], T.q_xx[:, a:e].bitcast(dt.uint8), ["q_xx%d" % hf], [])
+        act(T.yb[:, a:e], ps(hf, e - a), F.Copy, ["ps%d" % hf], ["yb%d" % hf])
+        dma("S", "y%d" % hf, T.y[:, a:e], T.yb[:, a:e], ["yb%d" % hf], [])
+    for i in range(4):
+        dma("Y" if i < 2 else "G", ("os0", "os1", "osg", "osg")[i], T.osc[4 * i:4 * i + 4, :], T.s_xx[32 * i:32 * i + 4, :], ["q_xx0", "q_xx1"], [])
+    for s, n in cnt.items():
+        if not any(seen[q].get(s, 0) >= n for q in Q):
+            (g if s in ("sent", "d_osg") else g.sync).wait_ge(T.sem[s], n)

@@ -1,9 +1,13 @@
+import numpy as np
 from concourse.mybir import dt, AluOpType as A, ActivationFunctionType as F
 
 C, H = 384, 192
 X4, U8, BF, F32, I32, U16 = "float8_e4m3fn_x4", "uint8", "bfloat16", "float32", "int32", "uint16"
-NS = (10, 7, 7)
+NS0 = 10
+VR = (3, 8)
 PW = 208
+S0, S1 = C + 2, H + 2
+HO = 2 * H
 BIG = 1.0e29
 
 SCRATCH = {}
@@ -18,24 +22,37 @@ _Q = dict(x=C, u=128, ur=128, v=128, w=512, e=512, lx=C, z0=H, z1=H, p1=H, p2=H,
 for _k, _n in _Q.items():
     _sb(X4, **{"q_" + _k: _n})
     _sb(U8, **{"s_" + _k: _n})
-_sb(BF, xb=4 * C, ub=512, vb=512, eb=2048, ones=128, ident=128,
-    m2=C, c16=416, c24=288, iob=PW, mval=H, d0=C, win=2 * 576, ww=2 * 576,
-    tpu=4 * C, tu8=4 * C, heldp=4 * 576, heldo=4 * 576, ztmp=4 * H,
+_sb(BF, xb=4 * C, ub=512, vb=512, eb=528, ones=528,
+    io16=C, m1=C, m2=C, c16=416, c24=288, iob=PW, iom=C, mval=H, d0=C, win1=576, win2=480, ww=2 * 576,
+    tpu=4 * C, tu8=4 * C, heldp=4 * 576, heldo=4 * HO, ztmp=4 * H,
     z0=4 * H, z1=4 * H, p1=4 * H, p2=4 * H, ee=4 * H, v2=4 * H, b1=4 * H, xx=4 * C,
     pv=12 * PW, x1=4 * C, x2=4 * C,
-    cmpv=24 * C, scv=24 * H, sig=24 * C, junk=24 * C, eq=C, tie=C, l1=576,
-    fb=224, ft=416, fts=416, mrow=448, mtt=832, o2row=PW, c1row=H, lc1=H,
+    cmpv=24 * C, scv=24 * H, sig0=NS0 * S0, eq=C, tie=C, l1=576,
+    fb=224, ft=416, fts=416, mrow=448, mtt=832, l0w=448, l0t=832, o2row=PW, c1row=H, lc1=H,
     ar=416 * 4, att=800 * 4)
-_sb(F32, io16=C, ior=C, m1=C, cols=8, jj=32, i16=32, s192=48, cb=48, tmp=160,
-    srow=C, prow=2 * H, msk=C, hh=C + 2 * H, a1=48, a2=48, tb=48, tb2=48, tb3=48, dd=48, rk=48, l0w=448, l0t=832,
-    ss=416, sst=816, ssw=32, spl=288, g1=128, cf=128, ucr=2 * C, yb=C)
+_sb(F32, ior=C, cols=8, jj=32, i16=32, s192=48, tmp=160, sig1=16 * S1, jlo=12 * S1, jup=12 * C,
+    srow=C, prow=2 * H, msk=C, hh=C + 2 * H, a1=48, a2=48, tb=64, rk=48,
+    ss=416, sst=816, ssw=32, spl=288 + H, g1=128, cf=160, ucr=C, yb=C)
 _sb(I32, pi=8, qi=32, hi=96)
-_sb(U16, uo=8, ko=52, rku=48, e0=32, o1=32, lst=112, le0=24, lo1=24, loff2=12, xo=128)
+_sb(U16, uo=8, ko=80, rku=48, e0=32, o1=32, lst=112, le0=24, lo1=24, loff2=12, xo=128)
 SCRATCH["ps"] = ("psum", [128, 4096], F32)
 
-_DMA = ["x0", "x1", "u", "wc", "ws", "v", "oc0", "oc1", "os0", "os1", "osg", "y0", "y1", "uc"]
+_DMA = ["x0", "x1", "u", "wc", "ws", "v", "out"]
 _REM = ["qx", "sx", "e0", "qp", "sp", "o1", "off2", "qv2", "sv2", "c1", "qb1", "sb1"]
 SEMAPHORES = ["cV", "cS", "cT", "cG", "sent"] + ["d_" + k for k in _DMA] + ["r_" + k for k in _REM]
+
+
+def R(name, a=0, n=None, step=1):
+    n = SCRATCH[name][1][1] - a if n is None else n
+    return (name, a, a + (n - 1) * step + 1, step, None)
+
+
+def pick(win, offs):
+    return win[:4] + (offs,)
+
+
+def sub(v, a, n):
+    return R(v[0], v[1] + a, n)
 
 
 def rank_program(g, core, T, topo):
@@ -47,465 +64,501 @@ def rank_program(g, core, T, topo):
     Q = {"V": g.vector, "S": g.scalar, "T": g.tensor, "G": g, "Y": g.sync}
     cnt, seen, wr, rd = {}, {q: {} for q in Q}, {}, {}
 
+    def ap(v):
+        if not isinstance(v, tuple):
+            return v
+        a = T[v[0]][:, v[1]:v[2]:v[3]] if v[3] > 1 else T[v[0]][:, v[1]:v[2]]
+        return a if v[4] is None else a.indirect(ap(v[4]))
+
+    def cols(v):
+        if v[0] == "ps":
+            return slice(v[1] // 512 * 512, v[1] // 512 * 512 + 512)
+        return slice(v[1], v[2], v[3])
+
+    def views(l):
+        l = [v for v in l if isinstance(v, tuple)]
+        return l + [v[4] for v in l if v[4] is not None]
+
     def need(q, r, w):
         deps = {}
-        for k in list(r) + list(w):
-            if k in wr:
-                deps[wr[k][0]] = max(deps.get(wr[k][0], 0), wr[k][1])
-        for k in w:
-            for s, n in rd.get(k, {}).items():
-                deps[s] = max(deps.get(s, 0), n)
-        for k in r:
-            if k.startswith("ps"):
-                for s, n in rd.get(k, {}).items():
-                    if s != "c" + q:
-                        deps[s] = max(deps.get(s, 0), n)
+        for tab, vs in ((wr, r + w), (rd, w), (rd, [v for v in r if v[0] == "ps"])):
+            for v in vs:
+                for s, last in tab.get(v[0], {}).items():
+                    if not (tab is rd and v[0] == "ps" and s == "c" + q):
+                        deps[s] = max(deps.get(s, 0), int(last[cols(v)].max()))
         for s, n in deps.items():
             if seen[q].get(s, 0) < n:
                 Q[q].wait_ge(T.sem[s], n)
                 seen[q][s] = n
 
     def mark(s, n, r, w):
-        for k in r:
-            rd.setdefault(k, {})[s] = n
-        for k in w:
-            wr[k] = (s, n)
-            rd[k] = {}
+        for tab, vs in ((rd, r), (wr, w)):
+            for v in vs:
+                if tab is wr:
+                    for t in (wr, rd):
+                        for last in t.get(v[0], {}).values():
+                            last[cols(v)] = 0
+                tab.setdefault(v[0], {}).setdefault(s, np.zeros(SCRATCH[v[0]][1][1], np.int64))[cols(v)] = n
 
     def op(q, fn, r, w):
+        r, w = views(r) + [v[4] for v in w if v[4] is not None], [v[:4] + (None,) for v in w]
         need(q, r, w)
         s = "c" + q
         cnt[s] = cnt.get(s, 0) + 1
         fn().then_inc(T.sem[s], 1)
         mark(s, cnt[s], r, w)
 
-    def dma(q, name, out, in_, r, w, **kw):
+    def dma(q, name, out, in_, r, w):
         need(q, r, w)
         s = "d_" + name
         cnt[s] = cnt.get(s, 0) + 16
-        Q[q].dma_start(out, in_, **kw).then_inc(T.sem[s], 16)
-        mark(s, cnt[s], r, w)
+        Q[q].dma_start(out, in_).then_inc(T.sem[s], 16)
+        if name != "out":
+            mark(s, cnt[s], r, w)
 
-    def send(name, dst, out, in_, r, land):
-        need("G", r, [])
+    def raw(v):
+        return ap(v).bitcast(dt.uint8) if SCRATCH[v[0]][2] == X4 else ap(v)
+
+    def send(name, dst, out, in_):
+        need("G", [in_], [])
         rid, pid, _ = topo.addr(dst)
-        g.remote_dma(out, in_, T.sem["r_" + name], T.sem.sent, pid, rid, topo.mask(core, dst))
+        g.remote_dma(raw(out), raw(in_), T.sem["r_" + name], T.sem.sent, pid, rid, topo.mask(core, dst))
         cnt["sent"] = cnt.get("sent", 0) + len(topo.engines(core, dst))
         src = prv if dst == nxt else nxt
         cnt["r_" + name] = len(topo.engines(src, core))
-        wr[land] = ("r_" + name, cnt["r_" + name])
+        mark("r_" + name, cnt["r_" + name], [], [out])
 
     def sendq(name, dst, a, b):
-        send("q" + name, dst, T["q_" + b][:].bitcast(dt.uint8), T["q_" + a][:].bitcast(dt.uint8), ["q_" + a], "q_" + b)
-        send("s" + name, dst, T["s_" + b][:], T["s_" + a][:], ["q_" + a], "s_" + b)
+        send("q" + name, dst, R("q_" + b), R("q_" + a))
+        send("s" + name, dst, R("s_" + b), R("s_" + a))
 
-    V, S, IO = g.vector, g.scalar, T.ior
+    V, S = g.vector, g.scalar
     fl = dict(allow_small_or_imprecise_dtypes=True)
 
-    def ts(out, in0, s1, op0, s2, op1, r, w):
-        if op1 is None:
-            op("V", lambda: V.tensor_scalar(out, in0, s1, None, op0), r, w)
-        else:
-            op("V", lambda: V.tensor_scalar(out, in0, s1, s2, op0, op1), r, w)
+    def ts(out, in0, s1, op0, s2=None, op1=None):
+        more = () if op1 is None else (op1,)
+        op("V", lambda: V.tensor_scalar(ap(out), ap(in0), ap(s1), ap(s2), op0, *more), [in0, s1, s2], [out])
 
-    def tt(out, in0, in1, o, r, w):
-        op("V", lambda: V.tensor_tensor(out, in0, in1, o), r, w)
+    def tt(out, in0, in1, o):
+        op("V", lambda: V.tensor_tensor(ap(out), ap(in0), ap(in1), o), [in0, in1], [out])
 
-    def cp(out, in_, r, w):
-        op("V", lambda: V.tensor_copy(out, in_), r, w)
+    def cp(out, in_):
+        op("V", lambda: V.tensor_copy(ap(out), ap(in_)), [in_], [out])
 
-    def ms(out, c, w):
-        op("V", lambda: V.memset(out, c), [], w)
+    def ms(out, c):
+        op("V", lambda: V.memset(ap(out), c), [], [out])
 
-    def gfill(out, n, c, w):
-        op("G", lambda: g.iota(out, [[0, n]], c, 0, **fl), [], w)
+    def iota(out, pattern, base, mult):
+        kw = {} if SCRATCH[out[0]][2] == I32 else fl
+        op("G", lambda: g.iota(ap(out), pattern, base, mult, **kw), [], [out])
 
-    def scan(out, d0, d1, o0, r, w):
-        op("V", lambda: V.tensor_tensor_scan(out, d0, d1, 0.0, o0, A.add), r, w)
+    def gfill(out, c, step=0):
+        iota(out, [[step, len(range(out[1], out[2], out[3]))]], c, 0)
 
-    def tr(out, in_, r, w):
-        op("V", lambda: V.transpose(out, in_), r, w)
+    def scan(out, d0, d1, o0, o1=A.add, init=0.0):
+        op("V", lambda: V.tensor_tensor_scan(ap(out), ap(d0), ap(d1), ap(init), o0, o1), [d0, d1, init], [out])
 
-    def act(out, in_, f, r, w, **kw):
-        op("S", lambda: S.activation(out, in_, f, **kw), r, w)
+    def tr(out, in_):
+        op("V", lambda: V.transpose(ap(out), ap(in_)), [in_], [out])
 
-    def quant(name, src, a=0, b=None, key=None, rk=None):
-        b = _Q[name] if b is None else b
-        op("V", lambda: V.quantize_mx(T["q_" + name][:, a:b], T["s_" + name][:, a:b], T[src][:, 4 * a:4 * b]),
-           rk or [src + str(i) for i in range(4)], [key or "q_" + name])
+    def act(out, in_, f, acc=None, **kw):
+        more = {k: ap(v) for k, v in kw.items()}
+        if acc is not None:
+            more["accum_out"] = ap(acc)
+        op("S", lambda: S.activation(ap(out), ap(in_), f, **more), [in_] + list(kw.values()), [out] + ([acc] if acc else []))
 
-    def mm(bank, st, c0, mv, a, b, r):
-        op("T", lambda: g.tensor.matmul_mx(T.ps[:, 512 * bank:512 * bank + b - a], T["q_" + st][:, c0:c0 + 128], T["s_" + st][:, c0:c0 + 128],
-                                           T["q_" + mv][:, a:b], T["s_" + mv][:, a:b], True, True), r, ["ps%d" % bank])
+    def sfill(out, c):
+        act(out, R("ones", 0, len(range(out[1], out[2], out[3]))), F.Identity, scale=0.0, bias=c)
 
-    def ps(bank, n):
-        return T.ps[:, 512 * bank:512 * bank + n]
+    def quant(name, src, a=0, n=None, s0=None):
+        n = _Q[name] if n is None else n
+        qo, so, in_ = R("q_" + name, a, n), R("s_" + name, a, n), R(src, 4 * a if s0 is None else s0, 4 * n)
+        op("V", lambda: V.quantize_mx(ap(qo), ap(so), ap(in_)), [in_], [qo, so])
+
+    def ps(bank, n, a=0):
+        return R("ps", 512 * bank + a, n)
+
+    def mm(bank, st, c0, mv, a, n):
+        ins = [R("q_" + st, c0, 128), R("s_" + st, c0, 128), R("q_" + mv, a, n), R("s_" + mv, a, n)]
+        op("T", lambda: g.tensor.matmul_mx(ap(ps(bank, n)), *[ap(v) for v in ins], True, True), ins, [ps(bank, n)])
 
     def four(st, mv, banks, n):
         for b in range(4):
-            mm(banks[b], st, 128 * b, mv, 0, n, ["q_" + st, "s_" + st, "q_" + mv, "s_" + mv])
+            mm(banks[b], st, 128 * b, mv, 0, n)
 
-    def evac(q, out, bank, n, scale, w):
+    def evac(q, out, bank, n, scale):
         if q == "V":
-            ts(out, ps(bank, n), scale, A.mult, None, None, ["ps%d" % bank], w)
+            ts(out, ps(bank, n), scale, A.mult)
         else:
-            act(out, ps(bank, n), F.Identity, ["ps%d" % bank], w, scale=scale)
+            act(out, ps(bank, n), F.Identity, scale=scale)
 
-    def to_tile(name, banks, scale):
-        for b, q in ((0, "V"), (1, "S"), (2, "V"), (3, "S")):
-            evac(q, T[name][:, b:4 * H:4], banks[b], H, scale, [name + str(b)])
+    def to_tile(name, banks, scale, qs="VSVS"):
+        for b in range(4):
+            evac(qs[b], R(name, b, H, 4), banks[b], H, scale)
 
-    KC, ODD, P208, P400, ODD1, K1024, EVEN = [T.cols[:, i:i + 1] for i in range(7)]
-    SELN, SELB, SELE, REP, SPLO = T.ko[:, 0:2], T.ko[:, 2:4], (T.ko[:, 4:6], T.ko[:, 6:8]), T.ko[:, 14:32], T.ko[:, 32:50]
-    SEL12 = [T.ko[:, 8 + 2 * i:9 + 2 * i] for i in range(3)]
-    O2, P1H, A0H, CU, OFF2 = T.lst[:, 0:12], T.lst[:, 36:48], T.lst[:, 48:72], T.lst[:, 72:96], T.lst[:, 96:108]
-    tm = lambda a, n: T.tmp[:, a:a + n]
-    A4, B4 = (2, 3, 4, 5), (6, 7, 6, 7)
+    KC, ODD, P208, P400, ODD1, K1024, EVEN, K16 = [R("cols", i, 1) for i in range(8)]
+    SELN, SELB, SELE = R("ko", 0, 2), R("ko", 2, 2), (R("ko", 4, 2), R("ko", 6, 2))
+    SEL12 = [R("ko", 8 + 2 * i, 1) for i in range(3)]
+    REP, SPLO = (None, R("ko", 14, 18), R("ko", 50, 12)), (None, R("ko", 32, 18), R("ko", 62, 12))
+    O2, P1H, A0H, CU, OFF2 = R("lst", 0, 12), R("lst", 36, 12), R("lst", 48, 24), R("lst", 72, 24), R("lst", 96, 12)
+    IO, RK0 = R("ior"), R("rku", 0, 24)
+    tm = lambda a, n: R("tmp", a, n)
+    jj = lambda n: R("jj", 0, n)
+    pi = lambda i, n=1: R("pi", i, n)
+    A4, B2 = (2, 3, 4, 5), (6, 7)
     OFS = (0, 24, 36)
+    SROWS = [m for m in range(12) if not VR[0] <= m < VR[1]]
 
-    dma("S", "u", T.ub[:], T.u[:], [], ["ub"])
-    dma("Y", "x0", T.xb[:, 0:768], T.x[:, 0:768], [], ["xb0"])
-    dma("Y", "x1", T.xb[:, 768:1536], T.x[:, 768:1536], [], ["xb1"])
-    dma("Y", "wc", T.q_w[:].bitcast(dt.uint8), T.wc[:], [], ["q_w"])
-    dma("Y", "ws", T.s_w[:], T.ws[:], [], ["s_w"])
-    dma("Y", "v", T.vb[:], T.v[:], [], ["vb"])
-    op("G", lambda: g.iota(T.pi[:, 0:1], [[0, 1]], 0, 1), [], ["pi0"])
-    op("G", lambda: g.iota(T.qi[:, 0:8], [[16, 8]], 0, 0), [], ["qi"])
-    ms(T.ones[:], 1.0, ["ones"])
-    op("G", lambda: g.iota(T.io16[:], [[0, 24], [1, 16]], 0, 0, **fl), [], ["io16"])
-    op("G", lambda: g.affine_select(T.ident[:], T.ones[:], [[-1, 128]], A.is_equal, 0.0, 0, 1), ["ones"], ["ident"])
-    op("G", lambda: g.iota(T.i16[:], [[16, 32]], 0, 0, **fl), [], ["i16"])
-    op("G", lambda: g.iota(IO[:], [[1, C]], 0, 0, **fl), [], ["io"])
-    ms(T.eb[:], 0.0, ["eb"])
-    ts(T.pi[:, 1:2], T.pi[:, 0:1], 4, A.arith_shift_right, None, None, ["pi0"], ["pi1"])
-    ts(T.pi[:, 4:5], T.pi[:, 0:1], 15, A.bitwise_and, None, None, ["pi0"], ["pi4"])
-    ts(T.pi[:, 5:6], T.pi[:, 0:1], 1, A.bitwise_and, None, None, ["pi0"], ["pi5"])
-    cp(T.uo[:], T.qi[:, 0:8], ["qi"], ["uo"])
-    ms(T.c16[:], 1.0, ["c16"])
-    tt(T.pi[:, 2:3], T.pi[:, 0:1], T.pi[:, 1:2], A.add, ["pi0", "pi1"], ["pi2"])
-    cp(T.cols[:, 0:2], T.pi[:, 4:6], ["pi4", "pi5"], ["col0"])
-    ms(T.c16[:, 0:416:16], 0.0, ["c16"])
-    ts(T.pi[:, 3:4], T.pi[:, 2:3], 1, A.bitwise_and, None, None, ["pi2"], ["pi3"])
-    ts(T.m1[:], T.io16[:], KC, A.is_equal, None, None, ["io16", "col0"], ["m1"])
-    ts(T.m2[:], T.io16[:], KC, A.is_gt, None, None, ["io16", "col0"], ["m2"])
-    for b in range(4):
-        act(T.eb[:, 512 * b + b:512 * b + 512:4], T.ident[:], F.Copy, ["ident", "eb"], ["eb%d" % b])
-    quant("u", "ub", rk=["ub"])
-    ts(P208, T.pi[:, 3:4], 208.0, A.mult, None, None, ["pi3"], ["col2"])
-    op("V", lambda: V.tensor_copy(T.q_ur[:].bitcast(dt.uint32), T.q_u[:].bitcast(dt.uint32).indirect(T.uo[:])), ["q_u", "uo"], ["q_ur"])
-    act(T.s_ur[:], T.s_u[:].indirect(T.uo[:]), F.Copy, ["q_u", "uo"], ["s_ur"])
-    quant("x", "xb", 0, H, "q_x0", ["xb0"])
-    quant("e", "eb", rk=["eb0", "eb1", "eb2", "eb3"])
-    quant("x", "xb", H, C, "q_x", ["xb1"])
-    mm(0, "ur", 0, "x", 0, C, ["q_ur", "s_ur", "q_x0", "q_x"])
-    mm(1, "ur", 0, "x", 0, C, ["q_ur", "s_ur", "q_x0", "q_x"])
+    dma("S", "u", T.ub[:], T.u[:], [], [R("ub")])
+    dma("Y", "x0", T.xb[:, 0:1024], T.x[:, 0:1024], [], [R("xb", 0, 1024)])
+    dma("Y", "x1", T.xb[:, 1024:1536], T.x[:, 1024:1536], [], [R("xb", 1024, 512)])
+    dma("Y", "wc", raw(R("q_w")), T.wc[:], [R("xb")], [R("q_w")])
+    dma("Y", "ws", T.s_w[:], T.ws[:], [], [R("s_w")])
+    dma("Y", "v", T.vb[:], T.v[:], [], [R("vb")])
+    iota(pi(0), [[0, 1]], 0, 1)
+    ms(R("ones"), 1.0)
+    iota(R("i16"), [[16, 32]], 0, 0)
+    iota(R("io16"), [[0, 24], [1, 16]], 0, 0)
+    op("G", lambda: g.affine_select(ap(R("eb")), ap(R("ones")), [[-1, 528]], A.is_equal, 0.0, 3, 4), [R("ones")], [R("eb")])
+    iota(IO, [[1, C]], 0, 0)
+    ms(R("c16"), 1.0)
+    ts(pi(1), pi(0), 4, A.arith_shift_right)
+    ts(pi(4), pi(0), 15, A.bitwise_and)
+    ts(pi(5), pi(0), 1, A.bitwise_and)
+    ms(R("c16", 0, 26, 16), 0.0)
+    tt(pi(2), pi(0), pi(1), A.add)
+    cp(R("cols", 0, 2), pi(4, 2))
+    cp(R("uo"), R("i16", 0, 8))
+    ts(pi(3), pi(2), 1, A.bitwise_and)
+    ts(jj(32), R("i16"), KC, A.add)
+    ts(ODD1, ODD, -1.0, A.add)
+    ts(K1024, ODD, 1024.0, A.mult)
+    ts(EVEN, ODD, -1.0, A.mult, 1.0, A.add)
+    ts(P208, pi(3), 208.0, A.mult)
+    ts(tm(0, 2), jj(2), 12.0, A.is_ge, 224.0, A.mult)
+    ts(P400, pi(3), 400.0, A.mult)
+    ts(tm(2, 2), jj(2), 16.0, A.mult, P208, A.add)
+    ts(R("m1"), R("io16"), KC, A.is_equal)
+    tt(tm(4, 2), tm(0, 2), tm(2, 2), A.add)
+    ts(R("m2"), R("io16"), KC, A.is_gt)
+    ts(SELE[0], tm(4, 2), 831.0, A.min)
+    for name, a, n in (("l0w", 0, 32), ("l0w", 416, 32), ("ss", 0, 16), ("ss", 400, 16), ("fb", 0, 16), ("fb", 208, 16),
+                       ("mrow", 0, 32), ("mrow", 416, 32)):
+        sfill(R(name, a, n), 0.0)
+    sfill(R("win1", 0, C), K1024)
+    sfill(R("win2", 0, H), K1024)
+    sfill(R("d0"), EVEN)
+    quant("u", "ub")
+    op("V", lambda: V.tensor_copy(T.q_ur[:].bitcast(dt.uint32), T.q_u[:].bitcast(dt.uint32).indirect(T.uo[:])),
+       [R("q_u"), R("uo")], [R("q_ur")])
+    act(R("s_ur"), pick(R("s_u"), R("uo")), F.Copy)
+    quant("x", "xb", 0, 256)
+    quant("x", "xb", 256, 128)
+    mm(0, "ur", 0, "x", 0, C)
+    mm(1, "ur", 0, "x", 0, C)
+    gfill(R("sig0", 0, NS0, S0), 16 - C, 16)
     sendq("x", nxt, "x", "lx")
-    ts(ODD1, ODD, -1.0, A.add, None, None, ["col0"], ["col4"])
-    ts(K1024, ODD, 1024.0, A.mult, None, None, ["col0"], ["col5"])
-    ts(EVEN, ODD, -1.0, A.mult, 1.0, A.add, ["col0"], ["col6"])
-    ts(T.jj[:], T.i16[:], KC, A.add, None, None, ["i16", "col0"], ["jj"])
-    for t, n in ((0, 24), (1, 12), (2, 12)):
-        o, ns = OFS[t], NS[t]
-        act(T.cb[:, o:o + ns], T.i16[:, 1:ns + 1], F.Copy, ["i16"], ["cb%d" % t])
-        act(T.cb[:, o + ns:o + n], T.i16[:, 0:n - ns], F.Identity, ["i16"], ["cb%db" % t], scale=0.0, bias=float(8 * n))
-    act(T.iob[:], IO[:, 0:PW], F.Copy, ["io"], ["iob"])
-    gfill(T.l0w[:, 0:32], 32, 0, ["l0p"])
-    gfill(T.l0w[:, 416:448], 32, 0, ["l0p2"])
-    gfill(T.ss[:, 0:16], 16, 0, ["ssp"])
-    gfill(T.ss[:, 400:416], 16, 0, ["ssp2"])
-    gfill(T.c24[:], 288, 1, ["c24"])
-    gfill(T.c24[:, 0:288:24], 12, 0, ["c24"])
-    gfill(T.fb[:], 224, 0, ["fb"])
-    gfill(T.mrow[:], 448, 0, ["mrow"])
-    gfill(T.ww[:], 2 * 576, 192, ["w1", "w2"])
-    gfill(T.ar[:], 4 * 416, 0, ["arp"])
-    gfill(T.o2row[:, H:PW], 16, 192, ["o2p"])
-    gfill(T.pv[:, H:12 * PW:PW], 12, 0, ["pvz"])
+    for b in range(4):
+        quant("e", "eb", 128 * b, 128, 3 - b)
+    act(R("iom"), IO, F.Identity, bias=-128.0)
+    act(R("mval"), R("ior", 0, H), F.Identity, scale=ODD, bias=ODD1)
+    gfill(R("c24"), 1)
+    gfill(R("c24", 0, 12, 24), 0)
+    gfill(R("sig1", 0, 12, S1), 16 - H, 16)
+    gfill(R("a1", 24, 24), 0)
+    gfill(R("tb"), 0)
+    iota(R("iob"), [[1, PW]], 0, 0)
+    gfill(R("ww", H, C), 192)
+    gfill(R("ww", 576 + H, C), 192)
+    for a, n in ((0, 16), (400, 32), (816, 32), (1232, 32), (1648, 16)):
+        gfill(R("ar", a, n), 0)
+    gfill(R("o2row", H, 16), 192)
+    gfill(R("pv", H, 12, PW), 0)
 
-    def sacc(m, n, o, tg):
+    def own_scores(hb, a, n):
+        tt(R("msk", a, n), ps(0, n, a), R("m1", a, n), A.mult)
+        return lambda: scan(R("hh", hb + a, n), R("c16", a, n), R("msk", a, n), A.mult)
+
+    def sign(sig, st, m, n, hb):
+        act(R(sig, st * m + 2, n), ps(1, n), F.Sign, scale=-1.0, bias=R("hh", hb + 16 * m + 15, 1))
+
+    def lower(sig, st, m, o):
         e = 16 * (m + 1)
-        act(T.junk[:, C * m:C * m + e], T.sig[:, C * m:C * m + e], F.Relu, ["sig%d" % m], ["jk%d" % m, "a1_%s%d" % (tg, m)],
-            scale=-1.0, accum_out=T.a1[:, o + m:o + m + 1])
-        act(T.junk[:, C * m + e:C * m + n], T.sig[:, C * m + e:C * m + n], F.Relu, ["sig%d" % m], ["jl%d" % m, "a2_%s%d" % (tg, m)],
-            accum_out=T.a2[:, o + m:o + m + 1])
+        act(R("jlo", S1 * m, e + 2), R(sig, st * m, e + 2), F.Relu, acc=R("a1", o + m, 1), scale=-1.0)
 
-    def ranking(t, n, row, hb, chain):
-        nm, tg, ns, o = n // 16, str(t), NS[t], OFS[t]
-        hh = T.hh[:, hb:hb + n]
-        act(row, ps(1, n), F.Copy, ["ps1"], ["row" + tg])
-        tt(T.msk[:, 0:n], ps(0, n), T.m1[:, 0:n], A.mult, ["ps0", "m1"], ["msk"])
-        scan(hh, T.c16[:, 0:n], T.msk[:, 0:n], A.mult, ["c16", "msk"], ["hh" + tg])
-        own = lambda m: T.hh[:, hb + 16 * m + 15:hb + 16 * m + 16]
-        for m in range(ns):
-            act(T.sig[:, C * m:C * m + n], row, F.Sign, ["row" + tg, "hh" + tg], ["sig%d" % m], scale=-1.0, bias=own(m))
-            if m > 0:
-                sacc(m - 1, n, o, tg)
-        sacc(ns - 1, n, o, tg)
-        fill = [lambda: tt(T.eq[:, 0:n], ps(0, n), hh, A.is_equal, ["ps0", "hh" + tg], ["eq"]),
-                lambda: scan(T.tie[:, 0:n], T.m2[:, 0:n], T.eq[:, 0:n], A.mult, ["m2", "eq"], ["tie"]),
-                lambda: tt(T.tb[:, o:o + nm], T.cb[:, o:o + nm], T.tie[:, 15:n:16], A.subtract, ["cb" + tg, "cb%sb" % tg, "tie"], ["tb" + tg])]
+    def upper(sig, st, m, n, o):
+        e = 16 * (m + 1)
+        if e < n:
+            act(R("jup", C * m, n - e), R(sig, st * m + 2 + e, n - e), F.Relu, acc=R("a2", o + m, 1))
 
-        def vrow(m):
-            e = 16 * (m + 1)
-            ts(T.cmpv[:, C * m:C * m + e], T.ps[:, 0:e], own(m), A.is_le, -0.5, A.add, ["ps0", "hh" + tg], ["cv%d" % m])
-            if e < n:
-                ts(T.cmpv[:, C * m + e:C * m + n], T.ps[:, e:n], own(m), A.is_lt, -0.5, A.add, ["ps0", "hh" + tg], ["cw%d" % m])
+    def vrow(m, n, hb, off):
+        e, own = 16 * (m + 1), R("hh", hb + 16 * m + 15, 1)
+        ts(R("cmpv", C * m, e), ps(0, e), own, A.is_le, off, A.add)
+        if e < n:
+            ts(R("cmpv", C * m + e, n - e), ps(0, n - e, e), own, A.is_lt, off, A.add)
 
-        def vsum(m):
-            h = n // 2
-            scan(T.scv[:, h * m:h * m + h], T.cmpv[:, C * m:C * m + h], T.cmpv[:, C * m + h:C * m + n], A.add, ["cv%d" % m, "cw%d" % m], ["sc%d" % m])
+    def vsum(m, n, init):
+        h = n // 2
+        scan(R("scv", h * m, h), R("cmpv", C * m, h), R("cmpv", C * m + h, h), A.add, init=init)
 
-        rows = []
-        for m in range(ns, nm):
-            rows.append(lambda m=m: (vrow(m), vsum(m - 1) if m > ns else None))
-        rows.append(lambda: vsum(nm - 1))
-        if chain:
-            order, rest = [], fill + rows
-            for c in chain:
-                order.append(c)
-                if rest:
-                    order.append(rest.pop(0))
-            order += rest
-        else:
-            order = [fill[0], rows[0], fill[1], rows[1], fill[2]] + rows[2:]
-        for f in order:
-            f()
-
-    def places(t, n, base, bkey):
-        nm, tg, h, ns, o = n // 16, str(t), n // 2, NS[t], OFS[t]
-        tt(T.dd[:, o:o + ns], T.a2[:, o:o + ns], T.a1[:, o:o + ns], A.subtract,
-           ["a%d_%s%d" % (i, tg, m) for m in range(ns) for i in (1, 2)], ["dd" + tg])
-        tt(T.rk[:, o + ns:o + nm], T.scv[:, h * ns + h - 1:h * nm:h], base[:, o + ns:o + nm], A.add,
-           ["sc%d" % m for m in range(ns, nm)] + [bkey], ["rkv" + tg])
-        tt(T.rk[:, o:o + ns], T.dd[:, o:o + ns], base[:, o:o + ns], A.add, ["dd" + tg, bkey], ["rks" + tg])
-        cp(T.rku[:, o:o + nm], T.rk[:, o:o + nm], ["rkv" + tg, "rks" + tg], ["rku" + tg])
-
-    def turn_eo(dst, src, r, w):
+    def turn_eo(dst, src):
         for o in (0, 1):
-            tr(dst[:, 416 * o:416 * o + H], src[:, 32 + o:32 + o + C - 1:2], r, [w + "a%d" % o])
-            tr(dst[:, 416 * o + H:416 * o + 416], src[:, o:o + 447:2], r, [w + "b%d" % o])
-        return [w + x for x in ("a0", "b0", "a1", "b1")]
+            tr(R(dst, 416 * o, H), R(src, 32 + o, H, 2))
+            tr(R(dst, 416 * o + H, 224), R(src, o, 224, 2))
 
-    def turn(dst, d0, src, s0, n, r, w):
-        tr(dst[:, d0:d0 + n], src[:, s0 + 16:s0 + 16 + n], r, [w + "a0"])
-        tr(dst[:, d0 + n:d0 + 2 * n + 32], src[:, s0:s0 + n + 32], r, [w + "b0"])
-        return [w + "a0", w + "b0"]
+    def turn(dst, d0, src, s0, n):
+        tr(R(dst, d0, n), R(src, s0 + 16, n))
+        tr(R(dst, d0 + n, n + 32), R(src, s0, n + 32))
 
-    def wrap_s(i, win, offs, r):
-        act(T.ar[:, 416 * i + 16:416 * i + 400], win.indirect(offs), F.Copy, r + ["arp"], ["ar%d" % i])
+    def wrap_s(i, win, offs):
+        act(R("ar", 416 * i + 16, C), pick(win, offs), F.Copy)
 
     def wrap_v(i):
-        kk = turn(T.att, 800 * i, T.ar, 416 * i, C, ["ar%d" % i], "att%d" % i)
-        cp(T.xo[:, 32 * i:32 * i + 32], T.att[:, 800 * i:800 * i + 800].indirect(SELN), kk + ["seln"], ["xo%d" % i])
-
-    def init_win(t):
-        a = 576 * (t - 1)
-        act(T.win[:, a:a + C], IO[:], F.Identity, ["io", "col5"], ["win%d" % t], scale=0.0, bias=K1024)
-        act(T.win[:, a + C:a + 576], IO[:, 0:H], F.Identity, ["io", "col5"], ["win%db" % t], scale=0.0, bias=K1024)
+        turn("att", 800 * i, "ar", 416 * i, C)
+        return lambda: cp(R("xo", 32 * i, 32), pick(R("att", 800 * i, 800), SELN))
 
     def sort_own(b):
         for o in range(2):
-            act(T.heldo[:, 576 * b + H + o:576 * b + 576:2], T.tu8[:, C * b:C * b + C].indirect(T.e0[:, 12 * o:12 * o + 12]), F.Copy,
-                ["tu8%d" % b, "e0"], ["ho%d%d" % (b, o)])
+            act(R("heldo", HO * b + H + o, 96, 2), pick(R("tu8", C * b, C), R("e0", 12 * o, 6)), F.Copy)
 
-    ranking(0, C, T.srow[:], 0, None)
-    ts(tm(0, 2), T.jj[:, 0:2], 12.0, A.is_ge, 224.0, A.mult, ["jj"], ["t0"])
-    ts(tm(2, 2), T.jj[:, 0:2], 16.0, A.mult, P208, A.add, ["jj", "col2"], ["t2"])
-    tt(tm(4, 2), tm(0, 2), tm(2, 2), A.add, ["t0", "t2"], ["t4"])
-    places(0, C, T.tb, "tb0")
+    def unpack_own(b):
+        mm(B2[b % 2], "e", 128 * b, "x", 0, C)
+        return lambda: evac("S", R("tu8", C * b, C), B2[b % 2], C, 0.125)
+
+    es = 16 * NS0
+    first = own_scores(0, 0, es)
+    rest = own_scores(0, es, C - es)
+    first()
+    rest()
+    sign("sig0", S0, 0, C, 0)
+    tt(R("eq"), ps(0, C), R("hh", 0, C), A.is_equal)
+    vrow(NS0, C, 0, -0.5)
+    scan(R("tie"), R("m2"), R("eq"), A.mult, A.subtract)
+    vrow(NS0 + 1, C, 0, -0.5)
+    cp(R("sig0", 1, NS0, S0), R("tie", 15, NS0, 16))
+    for m in range(NS0):
+        if m + 1 < NS0:
+            sign("sig0", S0, m + 1, C, 0)
+        upper("sig0", S0, m, C, 0)
+        lower("sig0", S0, m, 0)
+    for m in range(NS0, 24):
+        if m + 2 < 24:
+            vrow(m + 2, C, 0, -0.5)
+        vsum(m, C, R("tie", 16 * m + 15, 1))
+    act(R("srow"), ps(1, C), F.Copy)
     four("e", "lx", A4, C)
-    cp(T.l0w[:, 32:416].indirect(T.rku[:, 0:24]), IO[:], ["rku0", "io"], ["l0w"])
-    ts(SELE[0], tm(4, 2), 831.0, A.min, None, None, ["t4"], ["sele0"])
+    ts(tm(8, 2), jj(2), 24.0, A.is_ge, 1000.0, A.mult)
+    ts(R("rku", NS0, 24 - NS0), R("scv", H * NS0 + H - 1, 24 - NS0, H), C / 2, A.add)
+    ts(tm(6, 2), jj(2), 16.0, A.mult, P400, A.add)
+    cp(pick(R("l0w", 32, C), R("rku", NS0, 24 - NS0)), R("iom", es, C - es))
+    tt(R("rk", 0, NS0), R("a2", 0, NS0), R("a1", 0, NS0), A.subtract)
+    ts(tm(16, 18), jj(18), -11.5, A.add, 1.0 / 24.0, A.mult)
+    ts(R("rku", 0, NS0), R("rk", 0, NS0), float(C), A.add)
+    tt(tm(10, 2), tm(6, 2), tm(8, 2), A.add)
+    cp(pick(R("l0w", 32, C), R("rku", 0, NS0)), R("iom", 0, es))
     for b in range(4):
-        evac("S", T.tpu[:, C * b:C * b + C], A4[b], C, 0.5, ["tpu%d" % b])
-    k = turn_eo(T.l0t, T.l0w, ["l0w", "l0p", "l0p2"], "l0t")
-    cp(T.e0[:], T.l0t[:].indirect(SELE[0]), k + ["sele0"], ["e0"])
-    send("e0", nxt, T.le0[:], T.e0[:, 0:24], ["e0"], "le0")
-    for b in range(4):
-        mm(B4[b], "e", 128 * b, "x", 0, C, ["q_e", "q_x"])
-        if b < 3:
-            evac("S", T.tu8[:, C * b:C * b + C], B4[b], C, 0.125, ["tu8%d" % b])
+        evac("S", R("tpu", C * b, C), A4[b], C, 0.5)
+    cp(R("qi", 8, 18), tm(16, 18))
+    turn_eo("l0t", "l0w")
+    ts(SELB, tm(10, 2), 800.0, A.min)
+    ts(R("e0"), pick(R("l0t"), SELE[0]), 128.0, A.add)
+    send("e0", nxt, R("le0"), R("e0", 0, 24))
 
-    cp(T.ss[:, 16:400:2], T.srow[:].indirect(T.e0[:, 0:12]), ["row0", "e0"], ["ss0"])
-    act(T.ss[:, 17:400:2], T.srow[:].indirect(T.e0[:, 12:24]), F.Copy, ["row0", "e0"], ["ss1"])
-    ts(P400, T.pi[:, 3:4], 400.0, A.mult, None, None, ["pi3"], ["col3"])
-    ts(tm(8, 2), T.jj[:, 0:2], 24.0, A.is_ge, 1000.0, A.mult, ["jj"], ["t8"])
-    ts(tm(16, 18), T.jj[:, 0:18], -11.5, A.add, 1.0 / 24.0, A.mult, ["jj"], ["t16"])
-    ts(tm(6, 2), T.jj[:, 0:2], 16.0, A.mult, P400, A.add, ["jj", "col3"], ["t6"])
-    cp(T.qi[:, 8:26], tm(16, 18), ["t16"], ["qi8"])
-    ms(T.sst[:, 800:816], BIG, ["sstp"])
-    tt(tm(10, 2), tm(6, 2), tm(8, 2), A.add, ["t6", "t8"], ["t10"])
-    ts(tm(40, 18), T.qi[:, 8:26], -24.0, A.mult, None, None, ["qi8"], ["t40"])
-    k = turn(T.sst, 0, T.ss, 0, C, ["ssp", "ssp2", "ss0", "ss1"], "sst")
-    tt(tm(60, 18), tm(40, 18), T.jj[:, 0:18], A.add, ["t40", "jj"], ["t60"])
-    ts(SELB, tm(10, 2), 800.0, A.min, None, None, ["t10"], ["selb"])
-    ts(SPLO, tm(60, 18), 16.0, A.mult, 15.0, A.add, ["t60"], ["splo"])
-    ts(REP, T.qi[:, 8:26], 16.0, A.mult, 15.0, A.add, ["qi8"], ["rep"])
-    cp(T.ssw[:], T.sst[:].indirect(SELB), k + ["sstp", "selb"], ["ssw"])
-    ts(SELE[1], tm(4, 2), 1.0, A.add, 831.0, A.min, ["t4"], ["sele1"])
+    late = [unpack_own(0), unpack_own(1)]
+    ts(tm(40, 18), R("qi", 8, 18), -24.0, A.mult)
+    cp(R("ss", 16, H, 2), pick(R("srow"), R("e0", 0, 12)))
+    act(R("ss", 17, H, 2), pick(R("srow"), R("e0", 12, 12)), F.Copy)
+    tt(tm(60, 18), tm(40, 18), jj(18), A.add)
+    ms(R("sst", 800, 16), BIG)
+    ts(REP[1], R("qi", 8, 18), 16.0, A.mult, 15.0, A.add)
+    ts(SPLO[1], tm(60, 18), 16.0, A.mult, 15.0, A.add)
+    turn("sst", 0, "ss", 0, C)
     for i, r0 in enumerate((0.0, 1.0, 15.0)):
-        ts(SEL12[i], tm(2, 1), r0, A.add, 415.0, A.min, ["t2"], ["sel12%d" % i])
-    evac("S", T.tu8[:, C * 3:C * 4], B4[3], C, 0.125, ["tu83"])
-    init_win(1)
-    act(T.d0[:], IO[:], F.Identity, ["io", "col6"], ["d0"], scale=0.0, bias=EVEN)
-    act(T.mval[:], IO[:, 0:H], F.Identity, ["io", "col0", "col4"], ["mval"], scale=ODD, bias=ODD1)
+        ts(SEL12[i], tm(2, 1), r0, A.add, 415.0, A.min)
+    cp(R("ssw"), pick(R("sst"), SELB))
+    act(R("spl", 0, 288), pick(R("ss", 16, C), SPLO[1]), F.Copy)
+    late[0]()
+    late[1]()
+    ts(SELE[1], tm(4, 2), 1.0, A.add, 831.0, A.min)
+    ts(K16, KC, 16.0, A.mult, 15.0, A.add)
 
-    def zmake(t, win, stride, wkeys, lst, lkey, tmp, gaps, sgap):
-        z = "z%d" % t
+    def zmake(t, win, stride, lst, tmp, vgaps, sgaps):
+        z, p = "z%d" % t, "p%d" % (t + 1)
+        w = lambda b: R(win, stride * b, stride)
+        act(tmp(0, 0, 96), pick(w(0), R(lst, 12, 6)), F.Copy)
+        cp(tmp(0, 96, 96), pick(w(0), R(lst, 18, 6)))
         for b in range(4):
-            w = win[:, stride * b:stride * b + stride]
-            act(tmp(b), w.indirect(lst[:, 12:24]), F.Copy, wkeys(b) + [lkey], ["zt%d%d" % (t, b)])
-            tt(T[z][:, b:4 * H:4], w.indirect(lst[:, 0:12]), tmp(b), A.add, wkeys(b) + [lkey, "zt%d%d" % (t, b)], [z + str(b)])
+            if b > 0:
+                act(tmp(b, 0, H), pick(w(b), R(lst, 12, 12)), F.Copy)
+            tt(R(z, b, H, 4), pick(w(b), R(lst, 0, 12)), tmp(b, 0, H), A.add)
         quant(z, z)
-        sgap()
+        sgaps[0]()
         four("w", z, A4, H)
-        gaps[0]()
-        p = "p%d" % (t + 1)
+        vgaps[0]()
         to_tile(p, A4, 0.03125)
         quant(p, p)
-        mm(0, "ur", 0, p, 0, H, ["q_" + p])
-        mm(1, "ur", 0, p, 0, H, ["q_" + p])
-        gaps[1]()
+        mm(0, "ur", 0, p, 0, H)
+        mm(1, "ur", 0, p, 0, H)
+        vgaps[1]()
+        sgaps[1]()
 
-    def merge(t):
-        tg, o, hb = str(t), OFS[t], C + H * (t - 1)
-        row, bo = T.prow[:, H * (t - 1):H * t], T.lst[:, 12 * t:12 * t + 12]
-        ends = T.l1[:, 288 + 23:576:24]
-        chain = [
-            lambda: tt(T.l1[:, 0:288], T.hh[:, hb:hb + H].indirect(REP), T.spl[:], A.is_ge, ["hh" + tg, "rep", "spl"], ["l1"]),
-            lambda: scan(T.l1[:, 288:576], T.c24[:], T.l1[:, 0:288], A.mult, ["c24", "l1"], ["l1s"]),
-            lambda: cp(bo, ends, ["l1s"], ["bo" + tg]),
-            lambda: tt(T.fb[:, 16:208], T.ssw[:].indirect(bo), row, A.is_le, ["ssw", "bo" + tg, "row" + tg], ["fb"]),
-            lambda: (turn(T.ft, 0, T.fb, 0, H, ["fb"], "ft"),
-                     ts(T.tb2[:, o:o + 12], ends, 16.0, A.mult, None, None, ["l1s"], ["tb2" + tg])),
-            lambda: (scan(T.fts[:], T.c16[:], T.ft[:], A.mult, ["c16", "fta0", "ftb0"], ["fts"]),
-                     tt(T.tb3[:, o:o + 12], T.tb2[:, o:o + 12], T.tb[:, o:o + 12], A.add, ["tb2" + tg, "tb" + tg], ["tb3" + tg])),
-            lambda: cp(T.g1[:, 0:16], T.fts[:].indirect(SEL12[2]), ["fts", "sel122"], ["g1"]),
-            lambda: tt(T.tb2[:, o:o + 12], T.g1[:, 0:12], T.tb3[:, o:o + 12], A.add, ["g1", "tb3" + tg], ["tb2" + tg]),
-        ]
-        ranking(t, H, row, hb, chain)
-        places(t, H, T.tb2, "tb2" + tg)
+    def merge(t, win):
+        o, hb, nb = OFS[t], C + H * (t - 1), (None, 24, 16)[t]
+        row, bo, n1 = R("prow", H * (t - 1), H), R("lst", 12 * t, 12), 12 * nb
+        ends, extra = R("l1", 288 + nb - 1, 12, nb), R("sig1", 1, 16, S1)
+        own_scores(hb, 0, H)()
+        act(row, ps(1, H), F.Copy)
+        for m in SROWS:
+            sign("sig1", S1, m, H, hb)
+        tt(R("l1", 0, n1), pick(R("hh", hb, H), REP[t]), R("spl", 288 * (t - 1), n1), A.is_ge)
+        tt(R("eq", 0, H), ps(0, H), R("hh", hb, H), A.is_equal)
+        scan(R("l1", 288, n1), R(("c24", "c16")[t - 1], 0, n1), R("l1", 0, n1), A.mult)
+        scan(R("tie", 0, H), R("m2", 0, H), R("eq", 0, H), A.mult, A.subtract)
+        cp(bo, ends)
+        ts(R("tb", 0, 12), ends, 16.0, A.mult, -float(C), A.add)
+        tt(R("fb", 16, H), pick(R("ssw"), bo), row, A.is_le)
+        vrow(VR[0], H, hb, -1.0)
+        turn("ft", 0, "fb", 0, H)
+        tt(R("tb", 16, 12), R("tb", 0, 12), R("tie", 15, 12, 16), A.add)
+        vsum(VR[0], H, 0.0)
+        scan(R("fts"), R("c16"), R("ft"), A.mult)
+        vrow(VR[0] + 1, H, hb, -1.0)
+        tt(extra, pick(R("fts"), SEL12[2]), R("tb", 16, 16), A.add)
+        for m in SROWS:
+            upper("sig1", S1, m, H, o)
+        for m in SROWS:
+            lower("sig1", S1, m, o)
+        for m in range(VR[0] + 1, VR[1]):
+            if m + 1 < VR[1]:
+                vrow(m + 1, H, hb, -1.0)
+            vsum(m, H, 0.0)
+        nv = VR[1] - VR[0]
+        tt(R("a2", o + VR[0], nv), R("scv", 96 * VR[0] + 95, nv, 96), R("sig1", 1 + S1 * VR[0], nv, S1), A.add)
+        tt(R("rk", o, 12), R("a2", o, 12), R("a1", o, 12), A.subtract)
+        ts(R("rku", o, 12), R("rk", o, 12), float(C + H), A.add)
         if t == 2:
-            ts(OFF2, T.rk[:, 36:48], 192.0, A.min, None, None, ["rkv2", "rks2"], ["off2"])
-            send("off2", prv, T.loff2[:], OFF2, ["off2"], "loff2")
-        cp(T.win[:, 576 * (t - 1):576 * t].indirect(T.rku[:, o:o + 12]), T.mval[:], ["rku" + tg, "mval"], ["win" + tg, "win%sb" % tg])
+            ts(OFF2, R("rk", o, 12), float(C + H), A.add, 192.0, A.min)
+            send("off2", prv, R("loff2"), OFF2)
+        cp(pick(win, R("rku", o, 12)), R("mval"))
 
-    zmake(0, T.tpu, C, lambda b: ["tpu%d" % b], T.le0, "le0", lambda b: T.heldp[:, 576 * b + H + 1:576 * b + 576:2],
-          [lambda: (ts(tm(80, 32), T.jj[:], 192.0, A.is_ge, -383.0, A.mult, ["jj"], ["t80"]),
-                    ts(tm(112, 32), T.jj[:], 2.0, A.mult, 192.0, A.add, ["jj"], ["t112"])),
-           lambda: (tt(T.s192[:, 0:32], tm(80, 32), tm(112, 32), A.add, ["t80", "t112"], ["s192e"]),
-                    ts(SELN, tm(6, 2), 799.0, A.min, None, None, ["t6"], ["seln"]))],
-          lambda: act(T.spl[:], T.ss[:, 16:400].indirect(SPLO), F.Copy, ["ss0", "ss1", "splo"], ["spl"]))
+    def held_even(b):
+        act(R("heldp", 576 * b + H, H, 2), pick(R("tpu", C * b, C), R("le0", 0, 12)), F.Copy)
+
+    gfill(R("a2", OFS[1] + 11, 1), 0)
+    gfill(R("a2", OFS[2] + 11, 1), 0)
+    zmake(0, "tpu", C, "le0", lambda b, a, n: R("heldp", 576 * b + H + 1 + 2 * a, n, 2),
+          [lambda: (ts(tm(80, 32), jj(32), 192.0, A.is_ge, -383.0, A.mult), ts(tm(112, 32), jj(32), 2.0, A.mult, 192.0, A.add),
+                    ts(REP[2], R("i16", 0, 12), 15.0, A.add), ts(SPLO[2], R("i16", 0, 12), 0.0, A.mult, K16, A.add)),
+           lambda: (tt(R("s192", 0, 32), tm(80, 32), tm(112, 32), A.add), ts(SELN, tm(6, 2), 799.0, A.min))],
+          [lambda: (held_even(0), held_even(1)), lambda: None])
     sendq("p", nxt, "p1", "lp")
-    merge(1)
+    merge(1, R("win1"))
+    late = [unpack_own(2), unpack_own(3)]
     four("e", "lp", A4, H)
-    scan(T.mrow[:, 32:416], T.d0[:], T.win[:, 0:C], A.mult, ["d0", "win1"], ["mrow"])
+    cp(R("hi", 0, 36), R("rku", 0, 36))
+    scan(R("mrow", 32, C), R("d0"), R("win1", 0, C), A.mult)
+    held_even(2)
+    held_even(3)
     for b in range(4):
-        act(T.heldp[:, 576 * b + H:576 * b + 576:2], T.tpu[:, C * b:C * b + C].indirect(T.le0[:, 0:12]), F.Copy,
-            ["tpu%d" % b, "le0"], ["hpe%d" % b])
-    k = turn_eo(T.mtt, T.mrow, ["mrow"], "mtt")
-    tt(T.g1[:, 32:64], T.mtt[:].indirect(SELE[0]), T.s192[:, 0:32], A.add, k + ["sele0", "s192e"], ["g1b"])
-    tt(T.g1[:, 64:96], T.mtt[:].indirect(SELE[1]), T.g1[:, 32:64], A.min, k + ["sele1", "g1b"], ["g2b"])
-    cp(T.o1[:, 0:24], T.g1[:, 64:88], ["g2b"], ["o1"])
-    send("o1", nxt, T.lo1[:], T.o1[:, 0:24], ["o1"], "lo1")
+        evac("S", R("heldp", 576 * b, H), A4[b], H, 0.5)
+    turn_eo("mtt", "mrow")
+    ts(R("hi", 48, 36), R("hi", 0, 36), 1, A.arith_shift_right)
+    tt(R("g1", 32, 32), pick(R("mtt"), SELE[0]), R("s192", 0, 32), A.add)
+    tt(R("g1", 64, 32), pick(R("mtt"), SELE[1]), R("g1", 32, 32), A.min)
+    cp(R("o1", 0, 24), R("g1", 64, 24))
+    send("o1", nxt, R("lo1"), R("o1", 0, 24))
 
+    late[0]()
+    late[1]()
     for o in range(2):
-        cp(T.ww[:, 0:576].indirect(T.o1[:, 12 * o:12 * o + 12]), T.iob[:, 0:H], ["o1", "iob"], ["w1"])
-    for b in range(4):
-        evac("S", T.heldp[:, 576 * b:576 * b + H], A4[b], H, 0.5, ["hpp%d" % b])
-    sort_own(0)
-    sort_own(1)
-    wrap_s(3, T.ww[:, H:576], T.rku[:, 0:24], ["w1", "rku0"])
-    init_win(2)
-    cp(T.hi[:, 0:36], T.rk[:, 0:36], ["rkv0", "rks0", "rkv1", "rks1"], ["hi"])
-    quant("v", "vb", rk=["vb"])
-    ts(T.hi[:, 48:84], T.hi[:, 0:36], 1, A.arith_shift_right, None, None, ["hi"], ["hi2"])
-    wrap_v(3)
-    zmake(1, T.heldp, 576, lambda b: ["zt0%d" % b, "hpe%d" % b, "hpp%d" % b], T.lo1, "lo1", lambda b: T.ztmp[:, H * b:H * b + H],
-          [lambda: (ts(P1H, T.hi[:, 72:84], 192.0, A.min, None, None, ["hi2"], ["p1h"]),
-                    cp(A0H, T.hi[:, 48:72], ["hi2"], ["a0h"])),
-           lambda: ts(T.s192[:, 32:48], T.jj[:, 0:16], 192.0, A.add, None, None, ["jj"], ["s192n"])],
-          lambda: sort_own(2))
+        cp(pick(R("ww", 0, 576), R("o1", 12 * o, 12)), R("iob", 0, H))
+    act(R("spl", 288, H), pick(R("ss", 16, C), SPLO[2]), F.Copy)
+    wrap_s(3, R("ww", H, C), RK0)
+    quant("v", "vb")
+    late = []
+    zmake(1, "heldp", 576, "lo1", lambda b, a, n: R("ztmp", H * b + a, n),
+          [lambda: late.append(wrap_v(3)),
+           lambda: (late[0](), ts(R("s192", 32, 16), jj(16), 192.0, A.add))],
+          [lambda: (sort_own(0), sort_own(1)), lambda: None])
     four("e", "p2", A4, H)
-    merge(2)
-    scan(T.mrow[:, 32:32 + H], T.d0[:, 0:H], T.win[:, 576:576 + H], A.mult, ["d0", "win2"], ["mrow"])
+    merge(2, R("win2"))
+    scan(R("mrow", 32, H), R("d0", 0, H), R("win2", 0, H), A.mult)
     for b in range(4):
-        evac("S", T.heldo[:, 576 * b:576 * b + H], A4[b], H, 0.125, ["hop%d" % b])
+        evac("S", R("heldo", HO * b, H), A4[b], H, 0.125)
+    sort_own(2)
     sort_own(3)
-    k = turn(T.mtt, 0, T.mrow, 16, H, ["mrow"], "mtt")
-    tt(T.g1[:, 16:32], T.mtt[:, 0:416].indirect(SEL12[0]), T.s192[:, 32:48], A.add, k + ["sel120", "s192n"], ["g1c"])
-    tt(T.g1[:, 96:112], T.mtt[:, 0:416].indirect(SEL12[1]), T.g1[:, 16:32], A.min, k + ["sel121", "g1c"], ["g2"])
-    cp(O2, T.g1[:, 96:108], ["g2"], ["o2"])
+    ts(P1H, R("hi", 72, 12), 192.0, A.min)
+    turn("mtt", 0, "mrow", 16, H)
+    cp(A0H, R("hi", 48, 24))
+    tt(R("g1", 16, 16), pick(R("mtt", 0, 416), SEL12[0]), R("s192", 32, 16), A.add)
+    tt(R("g1", 96, 16), pick(R("mtt", 0, 416), SEL12[1]), R("g1", 16, 16), A.min)
+    cp(O2, R("g1", 96, 12))
     for b in (0, 2, 1, 3):
-        w, r = T.heldo[:, 576 * b:576 * b + 576].indirect(O2), ["hop%d" % b, "ho%d0" % b, "ho%d1" % b, "o2"]
+        w = pick(R("heldo", HO * b, HO), O2)
         if b < 2:
-            ts(T.ee[:, b:4 * H:4], w, 8.0, A.mult, None, None, r, ["ee%d" % b])
+            ts(R("ee", b, H, 4), w, 8.0, A.mult)
         else:
-            act(T.ee[:, b:4 * H:4], w, F.Identity, r, ["ee%d" % b], scale=8.0)
+            act(R("ee", b, H, 4), w, F.Identity, scale=8.0)
     quant("ee", "ee")
     four("w", "ee", A4, H)
-    to_tile("v2", A4, 0.03125)
+    cp(pick(R("ww", 576, 576), O2), R("iob", 0, H))
+    to_tile("v2", A4, 0.03125, "SSVS")
     quant("v2", "v2")
     sendq("v2", prv, "v2", "lb2")
 
-    def leaves(out, i, prev, b, a, e, r, w):
-        c0 = PW * (4 * i + b)
-        tt(out, T.pv[:, c0:c0 + PW].indirect(T.xo[:, 32 * i + a // 16:32 * i + e // 16]), T[prev][:, C * b + a:C * b + e], A.add,
-           r + ["xo%d" % i, "pvz", "pv%d%d" % (i, b)], w)
+    def leaves(out, i, prev, b, a, n):
+        tt(out, pick(R("pv", PW * (4 * i + b), PW), R("xo", 32 * i + a // 16, n // 16)), R(prev, C * b + a, n), A.add)
 
     def planes(i, b, scale):
-        c0 = PW * (4 * i + b)
-        evac("S", T.pv[:, c0:c0 + H], A4[b], H, scale, ["pv%d%d" % (i, b)])
+        evac("S", R("pv", PW * (4 * i + b), H), A4[b], H, scale)
 
-    act(T.o2row[:, 0:H], T.iob[:].indirect(T.loff2[:]), F.Copy, ["iob", "loff2"], ["o2row"])
-    wrap_s(1, T.o2row[:], T.xo[:, 96:120], ["o2row", "o2p", "xo3"])
-    cp(T.ww[:, 576:1152].indirect(O2), T.iob[:, 0:H], ["o2", "iob"], ["w2"])
-    wrap_s(0, T.ww[:, 576 + H:1152], T.rku[:, 0:24], ["w2", "rku0"])
+    wrap_s(0, R("ww", 576 + H, C), RK0)
     planes(0, 0, 0.03125 / 8)
-    act(T.c1row[:], T.o2row[:].indirect(P1H), F.Copy, ["o2row", "o2p", "p1h"], ["c1row"])
-    send("c1", prv, T.lc1[:], T.c1row[:], ["c1row"], "lc1")
-    for b in range(1, 4):
-        planes(0, b, 0.03125 / 8)
-    wrap_v(1)
-    wrap_v(0)
-    for b in range(3):
-        leaves(T.x1[:, C * b:C * b + C], 0, "tu8", b, 0, C, ["tu8%d" % b], ["x1%d" % b])
-        if b == 0:
-            ts(T.cf[:, 0:64], T.xo[:, 0:64], 192.0, A.is_lt, None, None, ["xo0", "xo1"], ["cf0"])
-        elif b == 1:
-            tt(T.cf[:, 96:120], T.cf[:, 0:24], T.cf[:, 32:56], A.add, ["cf0"], ["cf3"])
-        else:
-            cp(CU, T.cf[:, 96:120], ["cf3"], ["cu"])
+    wrap_v(0)()
+    planes(0, 1, 0.03125 / 8)
+    act(R("o2row", 0, H), pick(R("iob"), R("loff2")), F.Copy)
+    planes(0, 2, 0.03125 / 8)
+    planes(0, 3, 0.03125 / 8)
+    act(R("c1row"), pick(R("o2row"), P1H), F.Copy)
+    send("c1", prv, R("lc1"), R("c1row"))
+    wrap_s(1, R("o2row"), R("xo", 96, 24))
+    for b in range(4):
+        leaves(R("x1", C * b, C), 0, "tu8", b, 0, C)
+    wrap_v(1)()
     four("e", "lb2", A4, H)
-    to_tile("b1", A4, 1.0)
+    to_tile("b1", A4, 1.0, "SSSS")
     quant("b1", "b1")
     sendq("b1", prv, "b1", "lb1")
 
     for b in range(4):
         planes(1, b, 0.25)
-    wrap_s(2, T.lc1[:], A0H, ["lc1", "a0h"])
-    act(T.ucr[:, 0:C], IO[:, 0:16].indirect(CU), F.Copy, ["io", "cu"], ["ucr"])
-    dma("Y", "uc", T.uc[:], T.ucr[0:128:16, 0:C], ["ucr"], ["uc"])
-    act(T.ucr[:, C:2 * C], T.ar[:, 832 + 16:832 + 400], F.Sign, ["ar2"], ["ucr2"], scale=-1.0, bias=192.0)
-    dma("G", "osg", T.uc[:], T.ucr[0:128:16, C:2 * C], ["ucr2", "uc"], [], accum_op=A.add)
-    leaves(T.x1[:, C * 3:C * 4], 0, "tu8", 3, 0, C, ["tu83"], ["x13"])
+    wrap_s(2, R("lc1"), A0H)
     for b in range(4):
-        leaves(T.x2[:, C * b:C * b + C], 1, "x1", b, 0, C, ["x1%d" % b], ["x2%d" % b])
+        leaves(R("x2", C * b, C), 1, "x1", b, 0, C)
         if b == 1:
-            wrap_v(2)
+            late = wrap_v(2)
+        elif b == 2:
+            late()
+    ts(R("cf", 0, 96), R("xo", 0, 96), 192.0, A.is_lt)
+    tt(R("cf", 96, 24), R("cf", 0, 24), R("cf", 32, 24), A.add)
+    tt(R("cf", 128, 24), R("cf", 96, 24), R("cf", 64, 24), A.add)
+    cp(CU, R("cf", 128, 24))
     four("e", "lb1", A4, H)
     for b in range(4):
         planes(2, b, 0.5)
-    for hf, (a, e) in enumerate(((0, 256), (256, C))):
+    act(R("ucr"), pick(R("ior", 0, 16), CU), F.Copy)
+    dma("Y", "out", T.uc[:], T.ucr[0:128:16, :], [R("ucr")], [])
+    for hf, (a, n) in enumerate(((0, 256), (256, 128))):
         for b in range(4):
-            leaves(T.xx[:, 4 * a + b:4 * e:4], 2, "x2", b, a, e, ["x2%d" % b], ["xx%d%d" % (hf, b)])
-        quant("xx", "xx", a, e, "q_xx%d" % hf, ["xx%d%d" % (hf, b) for b in range(4)])
-        mm(hf, "v", 0, "xx", a, e, ["q_v", "q_xx%d" % hf])
-        dma("Y", "oc%d" % hf, T.oc[:, 4 * a:4 * e], T.q_xx[:, a:e].bitcast(dt.uint8), ["q_xx%d" % hf], [])
-        act(T.yb[:, a:e], ps(hf, e - a), F.Copy, ["ps%d" % hf], ["yb%d" % hf])
-        dma("S", "y%d" % hf, T.y[:, a:e], T.yb[:, a:e], ["yb%d" % hf], [])
-    for i in range(4):
-        dma("Y" if i < 2 else "G", ("os0", "os1", "osg", "osg")[i], T.osc[4 * i:4 * i + 4, :], T.s_xx[32 * i:32 * i + 4, :], ["q_xx0", "q_xx1"], [])
+            leaves(R("xx", 4 * a + b, n, 4), 2, "x2", b, a, n)
+        quant("xx", "xx", a, n)
+        mm(hf, "v", 0, "xx", a, n)
+        dma("Y", "out", T.oc[:, 4 * a:4 * (a + n)], raw(R("q_xx", a, n)), [R("q_xx", a, n)], [])
+        if hf == 1:
+            for i in range(4):
+                dma("YS"[i % 2], "out", T.osc[4 * i:4 * i + 4, :], T.s_xx[32 * i:32 * i + 4, :], [R("s_xx")], [])
+        act(R("yb", a, n), ps(hf, n), F.Copy)
+        dma("S", "out", T.y[:, a:a + n], T.yb[:, a:a + n], [R("yb", a, n)], [])
     for s, n in cnt.items():
         if not any(seen[q].get(s, 0) >= n for q in Q):
-            (g if s in ("sent", "d_osg") else g.sync).wait_ge(T.sem[s], n)
+            (g if s == "sent" else g.sync).wait_ge(T.sem[s], n)

@@ -3,56 +3,66 @@ from concourse.mybir import dt, AluOpType as A, ActivationFunctionType as F
 
 C, H = 384, 192
 X4, U8, BF, F32, I32, U16 = "float8_e4m3fn_x4", "uint8", "bfloat16", "float32", "int32", "uint16"
-NS0 = 10
+CUT0 = (0, 8, 18, 21, 24)
+R1 = CUT0[2]
 VR = (3, 8)
 PW = 208
 S0, S1 = C + 2, H + 2
 HO = 2 * H
 BIG = 1.0e29
 
-SCRATCH = {}
+SCRATCH, PART = {}, {"ps": ("ps", 0, 4096)}
 
 
 def _sb(dtype, **kw):
     for k, n in kw.items():
         SCRATCH[k] = ("sbuf", [128, n], dtype)
+        PART[k] = (k, 0, n)
 
 
-_Q = dict(x=C, u=128, ur=128, v=128, w=512, e=512, lx=C, z0=H, z1=H, p1=H, p2=H, lp=H, ee=H, v2=H, lb2=H, b1=H, lb1=H, xx=C)
+def _parts(buf, dtype, **kw):
+    a = 0
+    for k, n in kw.items():
+        PART[k] = (buf, a, n)
+        a += (n + 15) // 16 * 16
+    SCRATCH[buf] = ("sbuf", [128, a], dtype)
+
+
+_Q = dict(x=C, u=128, ur=128, v=128, w=512, e=512, lur=128, lx=C, z0=H, z1=H, p1=H, p2=H, lp=H, ee=H, v2=H, lb2=H, b1=H, lb1=H, xx=C)
 for _k, _n in _Q.items():
     _sb(X4, **{"q_" + _k: _n})
     _sb(U8, **{"s_" + _k: _n})
-_sb(BF, xb=4 * C, ub=512, vb=512, eb=528, ones=528,
-    io16=C, m1=C, m2=C, c16=416, c24=288, iob=PW, iom=C, mval=H, d0=C, win1=576, win2=480, ww=2 * 576,
+_sb(BF, xb=4 * C, ub=512, vb=512, eb=516, ones=516,
+    io16=256, m1=256, m2=256, mbig=C, c16=416, c24=288, iob=PW, iom=C, mval=H, d0=C, win1=576, win2=480, ww=2 * 576,
     tpu=4 * C, tu8=4 * C, heldp=4 * 576, heldo=4 * HO, ztmp=4 * H,
     z0=4 * H, z1=4 * H, p1=4 * H, p2=4 * H, ee=4 * H, v2=4 * H, b1=4 * H, xx=4 * C,
     pv=12 * PW, x1=4 * C, x2=4 * C,
-    cmpv=24 * C, scv=24 * H, sig0=NS0 * S0, eq=C, tie=C, l1=576,
-    fb=224, ft=416, fts=416, mrow=448, mtt=832, l0w=448, l0t=832, o2row=PW, c1row=H, lc1=H,
+    cmpv=24 * C, scv=24 * H, sc1=12 * 96, sig0=13 * S0, eq=C, tie=C, l1=576,
+    fb=224, ft=416, fts=416, mrow=448, mtt=832, l0w=448, l0t=832, o2row=PW, o3row=PW, c1row=H,
     ar=416 * 4, att=800 * 4)
-_sb(F32, ior=C, cols=8, jj=32, i16=32, s192=48, tmp=160, sig1=16 * S1, jlo=12 * S1, jup=12 * C,
-    srow=C, prow=2 * H, msk=C, hh=C + 2 * H, a1=48, a2=48, tb=64, rk=48,
-    ss=416, sst=816, ssw=32, spl=288 + H, g1=128, cf=160, ucr=C, yb=C)
+_parts("small", F32, cols=8, jj=32, i16=32, s192=48, tmp=160, a1=48, a2=48, tb=80, rk=48)
+_sb(BF, ior=H)
+_sb(F32, sig1=16 * S1, junk=8 * S0,
+    srow=C, prow=2 * H, msk=C, hh=C + 2 * H,
+    ss=C, ssw=C + 16, spl=288 + H, g1=128, cf=160, ucr=C, yb=C)
 _sb(I32, pi=8, qi=32, hi=96)
-_sb(U16, uo=8, ko=80, rku=48, e0=32, o1=32, lst=112, le0=24, lo1=24, loff2=12, xo=128)
+_sb(U16, uo=8, ko=80, rku=48, own=48, rkp=R1, rkl=56 - R1, o1=32, lst=112, lo1=24, loff2=12, loff3=12, lp1h=12, xo=128)
+PART["e0"], PART["e0p"] = ("own", 24, 24), ("rkl", 24 - R1, 24)
 SCRATCH["ps"] = ("psum", [128, 4096], F32)
 
 _DMA = ["x0", "x1", "u", "wc", "ws", "v", "out"]
-_REM = ["qx", "sx", "e0", "qp", "sp", "o1", "off2", "qv2", "sv2", "c1", "qb1", "sb1"]
-SEMAPHORES = ["cV", "cS", "cT", "cG", "sent"] + ["d_" + k for k in _DMA] + ["r_" + k for k in _REM]
+_REM = ["qu", "su", "qx", "sx", "rk", "e0", "qp", "sp", "o1", "p1h", "off2", "off3", "qv2", "sv2", "qb1", "sb1"]
+SEMAPHORES = ["cV", "cS", "cT", "cG", "sent", "sent0"] + ["d_" + k for k in _DMA] + ["r_" + k for k in _REM]
 
 
 def R(name, a=0, n=None, step=1):
-    n = SCRATCH[name][1][1] - a if n is None else n
-    return (name, a, a + (n - 1) * step + 1, step, None)
+    buf, a0, width = PART[name]
+    n = width - a if n is None else n
+    return (buf, a0 + a, a0 + a + (n - 1) * step + 1, step, None)
 
 
 def pick(win, offs):
     return win[:4] + (offs,)
-
-
-def sub(v, a, n):
-    return R(v[0], v[1] + a, n)
 
 
 def rank_program(g, core, T, topo):
@@ -60,7 +70,7 @@ def rank_program(g, core, T, topo):
     if rank is None:
         return
     N = len(T.cores)
-    nxt, prv = T.cores[(rank + 1) % N], T.cores[(rank - 1) % N]
+    nxt = T.cores[(rank + 1) % N]
     Q = {"V": g.vector, "S": g.scalar, "T": g.tensor, "G": g, "Y": g.sync}
     cnt, seen, wr, rd = {}, {q: {} for q in Q}, {}, {}
 
@@ -119,18 +129,19 @@ def rank_program(g, core, T, topo):
     def raw(v):
         return ap(v).bitcast(dt.uint8) if SCRATCH[v[0]][2] == X4 else ap(v)
 
-    def send(name, dst, out, in_):
+    def send(name, d, out, in_):
+        dst, src = T.cores[(rank + d) % N], T.cores[(rank - d) % N]
         need("G", [in_], [])
         rid, pid, _ = topo.addr(dst)
-        g.remote_dma(raw(out), raw(in_), T.sem["r_" + name], T.sem.sent, pid, rid, topo.mask(core, dst))
-        cnt["sent"] = cnt.get("sent", 0) + len(topo.engines(core, dst))
-        src = prv if dst == nxt else nxt
+        left = "sent0" if name in _REM[:5] else "sent"
+        g.remote_dma(raw(out), raw(in_), T.sem["r_" + name], T.sem[left], pid, rid, topo.mask(core, dst))
+        cnt[left] = cnt.get(left, 0) + len(topo.engines(core, dst))
         cnt["r_" + name] = len(topo.engines(src, core))
         mark("r_" + name, cnt["r_" + name], [], [out])
 
-    def sendq(name, dst, a, b):
-        send("q" + name, dst, R("q_" + b), R("q_" + a))
-        send("s" + name, dst, R("s_" + b), R("s_" + a))
+    def sendq(name, d, a, b):
+        for k in "qs":
+            send(k + name, d, R(k + "_" + b), R(k + "_" + a))
 
     V, S = g.vector, g.scalar
     fl = dict(allow_small_or_imprecise_dtypes=True)
@@ -167,13 +178,21 @@ def rank_program(g, core, T, topo):
             more["accum_out"] = ap(acc)
         op("S", lambda: S.activation(ap(out), ap(in_), f, **more), [in_] + list(kw.values()), [out] + ([acc] if acc else []))
 
+    def lin(out, in_, scale, bias):
+        act(out, in_, F.Identity, scale=scale, bias=bias)
+
     def sfill(out, c):
-        act(out, R("ones", 0, len(range(out[1], out[2], out[3]))), F.Identity, scale=0.0, bias=c)
+        lin(out, R("ones", 0, len(range(out[1], out[2], out[3]))), 0.0, c)
 
     def quant(name, src, a=0, n=None, s0=None):
         n = _Q[name] if n is None else n
         qo, so, in_ = R("q_" + name, a, n), R("s_" + name, a, n), R(src, 4 * a if s0 is None else s0, 4 * n)
         op("V", lambda: V.quantize_mx(ap(qo), ap(so), ap(in_)), [in_], [qo, so])
+
+    def pickq(name, src, offs):
+        qo, qi = R("q_" + name), R("q_" + src)
+        op("V", lambda: V.tensor_copy(ap(qo).bitcast(dt.uint32), ap(qi).bitcast(dt.uint32).indirect(ap(offs))), [qi, offs], [qo])
+        act(R("s_" + name), pick(R("s_" + src), offs), F.Copy)
 
     def ps(bank, n, a=0):
         return R("ps", 512 * bank + a, n)
@@ -192,16 +211,16 @@ def rank_program(g, core, T, topo):
         else:
             act(out, ps(bank, n), F.Identity, scale=scale)
 
-    def to_tile(name, banks, scale, qs="VSVS"):
+    def to_tile(name, banks, scale, qs):
         for b in range(4):
             evac(qs[b], R(name, b, H, 4), banks[b], H, scale)
 
     KC, ODD, P208, P400, ODD1, K1024, EVEN, K16 = [R("cols", i, 1) for i in range(8)]
-    SELN, SELB, SELE = R("ko", 0, 2), R("ko", 2, 2), (R("ko", 4, 2), R("ko", 6, 2))
+    SELN, SELE = R("ko", 0, 2), (R("ko", 4, 2), R("ko", 6, 2))
     SEL12 = [R("ko", 8 + 2 * i, 1) for i in range(3)]
     REP, SPLO = (None, R("ko", 14, 18), R("ko", 50, 12)), (None, R("ko", 32, 18), R("ko", 62, 12))
     O2, P1H, A0H, CU, OFF2 = R("lst", 0, 12), R("lst", 36, 12), R("lst", 48, 24), R("lst", 72, 24), R("lst", 96, 12)
-    IO, RK0 = R("ior"), R("rku", 0, 24)
+    RK0 = R("own", 0, 24)
     tm = lambda a, n: R("tmp", a, n)
     jj = lambda n: R("jj", 0, n)
     pi = lambda i, n=1: R("pi", i, n)
@@ -212,15 +231,11 @@ def rank_program(g, core, T, topo):
     dma("S", "u", T.ub[:], T.u[:], [], [R("ub")])
     dma("Y", "x0", T.xb[:, 0:1024], T.x[:, 0:1024], [], [R("xb", 0, 1024)])
     dma("Y", "x1", T.xb[:, 1024:1536], T.x[:, 1024:1536], [], [R("xb", 1024, 512)])
-    dma("Y", "wc", raw(R("q_w")), T.wc[:], [R("xb")], [R("q_w")])
-    dma("Y", "ws", T.s_w[:], T.ws[:], [], [R("s_w")])
-    dma("Y", "v", T.vb[:], T.v[:], [], [R("vb")])
     iota(pi(0), [[0, 1]], 0, 1)
     ms(R("ones"), 1.0)
     iota(R("i16"), [[16, 32]], 0, 0)
-    iota(R("io16"), [[0, 24], [1, 16]], 0, 0)
-    op("G", lambda: g.affine_select(ap(R("eb")), ap(R("ones")), [[-1, 528]], A.is_equal, 0.0, 3, 4), [R("ones")], [R("eb")])
-    iota(IO, [[1, C]], 0, 0)
+    iota(R("io16"), [[0, 16], [1, 16]], 0, 0)
+    op("G", lambda: g.affine_select(ap(R("eb")), ap(R("ones")), [[-1, 516]], A.is_equal, 0.0, 3, 4), [R("ones")], [R("eb")])
     ms(R("c16"), 1.0)
     ts(pi(1), pi(0), 4, A.arith_shift_right)
     ts(pi(4), pi(0), 15, A.bitwise_and)
@@ -228,78 +243,77 @@ def rank_program(g, core, T, topo):
     ms(R("c16", 0, 26, 16), 0.0)
     tt(pi(2), pi(0), pi(1), A.add)
     cp(R("cols", 0, 2), pi(4, 2))
-    cp(R("uo"), R("i16", 0, 8))
+    cp(R("uo", 0, 8), R("i16", 0, 8))
     ts(pi(3), pi(2), 1, A.bitwise_and)
     ts(jj(32), R("i16"), KC, A.add)
-    ts(ODD1, ODD, -1.0, A.add)
+    scan(R("ior"), R("ones", 0, H), R("ones", 0, H), A.mult)
     ts(K1024, ODD, 1024.0, A.mult)
     ts(EVEN, ODD, -1.0, A.mult, 1.0, A.add)
     ts(P208, pi(3), 208.0, A.mult)
     ts(tm(0, 2), jj(2), 12.0, A.is_ge, 224.0, A.mult)
-    ts(P400, pi(3), 400.0, A.mult)
     ts(tm(2, 2), jj(2), 16.0, A.mult, P208, A.add)
     ts(R("m1"), R("io16"), KC, A.is_equal)
     tt(tm(4, 2), tm(0, 2), tm(2, 2), A.add)
     ts(R("m2"), R("io16"), KC, A.is_gt)
     ts(SELE[0], tm(4, 2), 831.0, A.min)
-    for name, a, n in (("l0w", 0, 32), ("l0w", 416, 32), ("ss", 0, 16), ("ss", 400, 16), ("fb", 0, 16), ("fb", 208, 16),
-                       ("mrow", 0, 32), ("mrow", 416, 32)):
+    for name, a, n in (("l0w", 0, 32), ("l0w", 416, 32), ("fb", 0, 16), ("fb", 208, 16), ("mrow", 0, 32), ("mrow", 416, 32)):
         sfill(R(name, a, n), 0.0)
     sfill(R("win1", 0, C), K1024)
     sfill(R("win2", 0, H), K1024)
     sfill(R("d0"), EVEN)
     quant("u", "ub")
-    op("V", lambda: V.tensor_copy(T.q_ur[:].bitcast(dt.uint32), T.q_u[:].bitcast(dt.uint32).indirect(T.uo[:])),
-       [R("q_u"), R("uo")], [R("q_ur")])
-    act(R("s_ur"), pick(R("s_u"), R("uo")), F.Copy)
+    pickq("ur", "u", R("uo"))
+    sendq("u", 1, "ur", "lur")
+    quant("e", "eb", 0, 128, 3)
+    quant("e", "eb", 128, 128, 2)
+    ts(P400, pi(3), 400.0, A.mult)
+    ts(SELE[1], tm(4, 2), 1.0, A.add, 831.0, A.min)
     quant("x", "xb", 0, 256)
+    mm(2, "ur", 0, "x", 0, 256)
+    quant("e", "eb", 256, 128, 1)
     quant("x", "xb", 256, 128)
-    mm(0, "ur", 0, "x", 0, C)
     mm(1, "ur", 0, "x", 0, C)
-    gfill(R("sig0", 0, NS0, S0), 16 - C, 16)
-    sendq("x", nxt, "x", "lx")
-    for b in range(4):
-        quant("e", "eb", 128 * b, 128, 3 - b)
-    act(R("iom"), IO, F.Identity, bias=-128.0)
-    act(R("mval"), R("ior", 0, H), F.Identity, scale=ODD, bias=ODD1)
-    gfill(R("c24"), 1)
-    gfill(R("c24", 0, 12, 24), 0)
-    gfill(R("sig1", 0, 12, S1), 16 - H, 16)
-    gfill(R("a1", 24, 24), 0)
-    gfill(R("tb"), 0)
-    iota(R("iob"), [[1, PW]], 0, 0)
-    gfill(R("ww", H, C), 192)
-    gfill(R("ww", 576 + H, C), 192)
-    for a, n in ((0, 16), (400, 32), (816, 32), (1232, 32), (1648, 16)):
-        gfill(R("ar", a, n), 0)
-    gfill(R("o2row", H, 16), 192)
-    gfill(R("pv", H, 12, PW), 0)
+    mm(0, "ur", 0, "x", 0, C)
+    sendq("x", 1, "x", "lx")
+    for a in (0, H):
+        lin(R("mbig", a, H), R("m1", 0, H), 2 * BIG, -BIG)
+    slot = 0
+    for a, e in zip(CUT0[0::2], CUT0[1::2]):
+        lin(R("sig0", S0 * slot, e - a, S0), R("i16", a, e - a), 1.0, 16.0 - C)
+        slot += e - a
+    lin(R("mval"), R("ior"), ODD, -1.0)
+    lin(tm(16, 18), jj(18), 1.0 / 24.0, -11.5 / 24.0)
+    lin(tm(6, 2), jj(2), 16.0, P400)
+    lin(K16, KC, 16.0, 15.0)
+    lin(tm(112, 32), jj(32), 2.0, 192.0)
+    lin(R("s192", 32, 16), jj(16), 1.0, 192.0)
+    iota(R("iom"), [[1, C]], -128, 0)
 
-    def own_scores(hb, a, n):
-        tt(R("msk", a, n), ps(0, n, a), R("m1", a, n), A.mult)
+    def own_scores(hb, a, n, bank):
+        tt(R("msk", a, n), ps(bank, n, a), R("m1", 0, n), A.mult)
         return lambda: scan(R("hh", hb + a, n), R("c16", a, n), R("msk", a, n), A.mult)
 
-    def sign(sig, st, m, n, hb):
-        act(R(sig, st * m + 2, n), ps(1, n), F.Sign, scale=-1.0, bias=R("hh", hb + 16 * m + 15, 1))
+    def sign(sig, st, i, m, n, hb, bank):
+        act(R(sig, st * i + 2, n), ps(bank, n), F.Sign, scale=-1.0, bias=R("hh", hb + 16 * m + 15, 1))
 
-    def lower(sig, st, m, o):
+    def lower(sig, st, i, m, o):
         e = 16 * (m + 1)
-        act(R("jlo", S1 * m, e + 2), R(sig, st * m, e + 2), F.Relu, acc=R("a1", o + m, 1), scale=-1.0)
+        act(R("junk", S0 * (i % 4), e + 2), R(sig, st * i, e + 2), F.Relu, acc=R("a1", o + m, 1), scale=-1.0)
 
-    def upper(sig, st, m, n, o):
+    def upper(sig, st, i, m, n, o):
         e = 16 * (m + 1)
         if e < n:
-            act(R("jup", C * m, n - e), R(sig, st * m + 2 + e, n - e), F.Relu, acc=R("a2", o + m, 1))
+            act(R("junk", S0 * (4 + i % 4), n - e), R(sig, st * i + 2 + e, n - e), F.Relu, acc=R("a2", o + m, 1))
 
-    def vrow(m, n, hb, off):
+    def vrow(m, n, hb, off, bank=0):
         e, own = 16 * (m + 1), R("hh", hb + 16 * m + 15, 1)
-        ts(R("cmpv", C * m, e), ps(0, e), own, A.is_le, off, A.add)
+        ts(R("cmpv", n * m, e), ps(bank, e), own, A.is_le, off, A.add)
         if e < n:
-            ts(R("cmpv", C * m + e, n - e), ps(0, n - e, e), own, A.is_lt, off, A.add)
+            ts(R("cmpv", n * m + e, n - e), ps(bank, n - e, e), own, A.is_lt, off, A.add)
 
     def vsum(m, n, init):
         h = n // 2
-        scan(R("scv", h * m, h), R("cmpv", C * m, h), R("cmpv", C * m + h, h), A.add, init=init)
+        scan(R("scv" if n == C else "sc1", h * m, h), R("cmpv", n * m, h), R("cmpv", n * m + h, h), A.add, init=init)
 
     def turn_eo(dst, src):
         for o in (0, 1):
@@ -325,64 +339,98 @@ def rank_program(g, core, T, topo):
         mm(B2[b % 2], "e", 128 * b, "x", 0, C)
         return lambda: evac("S", R("tu8", C * b, C), B2[b % 2], C, 0.125)
 
-    es = 16 * NS0
-    first = own_scores(0, 0, es)
-    rest = own_scores(0, es, C - es)
+    def ties(bank, a, n):
+        tt(R("eq", a, n), ps(bank, n, a), R("hh", a, n), A.is_equal)
+        return lambda: scan(R("tie", a, n), R("m2", 0, n), R("eq", a, n), A.mult, A.subtract)
+
+    def srows(rows, slot, bank):
+        for i in range(len(rows) + 2):
+            if 0 < i + 1 < len(rows):
+                sign("sig0", S0, slot + i + 1, rows[i + 1], C, 0, bank)
+            if i < len(rows):
+                upper("sig0", S0, slot + i, rows[i], C, 0)
+            if i >= 2:
+                lower("sig0", S0, slot + i - 2, rows[i - 2], 0)
+
+    def vrows(rows, bank, after={}):
+        for i, m in enumerate(rows):
+            if i + 2 < len(rows):
+                vrow(rows[i + 2], C, 0, -0.5, bank)
+            vsum(m, C, R("tie", 16 * m + 15, 1))
+            if m in after:
+                after[m]()
+
+    def splaces(out, rows, fill):
+        tt(R("rk", rows[0], len(rows)), R("a2", rows[0], len(rows)), R("a1", rows[0], len(rows)), A.subtract)
+        fill()
+        ts(out, R("rk", rows[0], len(rows)), float(C), A.add)
+
+    def vplaces(out, rows):
+        ts(out, R("scv", H * rows[0] + H - 1, len(rows), H), C / 2, A.add)
+
+    sa, va, sb, vb = [list(range(a, e)) for a, e in zip(CUT0[:-1], CUT0[1:])]
+    eh = 16 * R1
+    first = own_scores(0, 0, 16 * len(sa), 2)
+    rest = own_scores(0, 16 * len(sa), 256 - 16 * len(sa), 2)
     first()
     rest()
-    sign("sig0", S0, 0, C, 0)
-    tt(R("eq"), ps(0, C), R("hh", 0, C), A.is_equal)
-    vrow(NS0, C, 0, -0.5)
-    scan(R("tie"), R("m2"), R("eq"), A.mult, A.subtract)
-    vrow(NS0 + 1, C, 0, -0.5)
-    cp(R("sig0", 1, NS0, S0), R("tie", 15, NS0, 16))
-    for m in range(NS0):
-        if m + 1 < NS0:
-            sign("sig0", S0, m + 1, C, 0)
-        upper("sig0", S0, m, C, 0)
-        lower("sig0", S0, m, 0)
-    for m in range(NS0, 24):
-        if m + 2 < 24:
-            vrow(m + 2, C, 0, -0.5)
-        vsum(m, C, R("tie", 16 * m + 15, 1))
-    act(R("srow"), ps(1, C), F.Copy)
+    sign("sig0", S0, 0, 0, C, 0, 1)
+    late = ties(2, 0, 256)
+    quant("e", "eb", 384, 128, 0)
+    late()
+    late = own_scores(0, 256, eh - 256, 0) if eh > 256 else lambda: None
+    cp(R("sig0", 1, len(sa), S0), R("tie", 15, len(sa), 16))
+    late()
+    vrow(va[0], C, 0, -0.5, 0)
+    late = ties(0, 256, eh - 256) if eh > 256 else lambda: None
+    vrow(va[1], C, 0, -0.5, 0)
+    late()
+    srows(sa, 0, 1)
+    mm(6, "lur", 0, "lx", 0, C)
+    mm(7, "lur", 0, "lx", 0, C)
+    late = []
+    vrows(va, 0, {va[-3]: lambda: late.append(own_scores(0, eh, C - eh, 6)), va[-2]: lambda: late[0]()})
+    splaces(R("own", 0, len(sa)), sa, lambda: vplaces(R("own", va[0], len(va)), va))
+    send("rk", 1, R("rkp", 0, R1), R("own", 0, R1))
+    g.sync.wait_ge(T.sem.sent0, cnt["sent0"])
+    seen["Y"]["sent0"] = cnt["sent0"]
+    dma("Y", "wc", raw(R("q_w")), T.wc[:], [], [R("q_w")])
+    dma("Y", "ws", T.s_w[:], T.ws[:], [], [R("s_w")])
+    dma("Y", "v", T.vb[:], T.v[:], [], [R("vb")])
     four("e", "lx", A4, C)
-    ts(tm(8, 2), jj(2), 24.0, A.is_ge, 1000.0, A.mult)
-    ts(R("rku", NS0, 24 - NS0), R("scv", H * NS0 + H - 1, 24 - NS0, H), C / 2, A.add)
-    ts(tm(6, 2), jj(2), 16.0, A.mult, P400, A.add)
-    cp(pick(R("l0w", 32, C), R("rku", NS0, 24 - NS0)), R("iom", es, C - es))
-    tt(R("rk", 0, NS0), R("a2", 0, NS0), R("a1", 0, NS0), A.subtract)
-    ts(tm(16, 18), jj(18), -11.5, A.add, 1.0 / 24.0, A.mult)
-    ts(R("rku", 0, NS0), R("rk", 0, NS0), float(C), A.add)
-    tt(tm(10, 2), tm(6, 2), tm(8, 2), A.add)
-    cp(pick(R("l0w", 32, C), R("rku", 0, NS0)), R("iom", 0, es))
+    slot = len(sa)
+    sign("sig0", S0, slot, sb[0], C, 0, 7)
+    late = ties(6, eh, C - eh)
+    vrow(vb[0], C, 0, -0.5, 6)
+    late()
+    vrow(vb[1], C, 0, -0.5, 6)
+    cp(R("sig0", 1 + S0 * slot, len(sb), S0), R("tie", 16 * sb[0] + 15, len(sb), 16))
+    srows(sb, slot, 7)
+    vrows(vb, 6)
+    gfill(R("c24"), 1)
+    gfill(R("c24", 0, 12, 24), 0)
+    gfill(R("sig1", 0, 12, S1), 16 - H, 16)
+    gfill(R("sig1", 1, 12, S1), 0)
+    gfill(R("a1", 24, 24), 0)
+    gfill(R("a2", 24, 24), 0)
+    gfill(R("sc1", 95, 12, 96), 0)
+    gfill(R("tb", 16, 16), 0)
+    cp(pick(R("l0w", 32, C), R("rkp", 0, R1)), R("iom", 0, eh))
+    splaces(R("rkl", 0, len(sb)), sb, lambda: vplaces(R("rkl", len(sb), len(vb)), vb))
     for b in range(4):
         evac("S", R("tpu", C * b, C), A4[b], C, 0.5)
     cp(R("qi", 8, 18), tm(16, 18))
-    turn_eo("l0t", "l0w")
-    ts(SELB, tm(10, 2), 800.0, A.min)
-    ts(R("e0"), pick(R("l0t"), SELE[0]), 128.0, A.add)
-    send("e0", nxt, R("le0"), R("e0", 0, 24))
-
-    late = [unpack_own(0), unpack_own(1)]
+    cp(pick(R("l0w", 32, C), R("rkl", 0, 24 - R1)), R("iom", eh, C - eh))
     ts(tm(40, 18), R("qi", 8, 18), -24.0, A.mult)
-    cp(R("ss", 16, H, 2), pick(R("srow"), R("e0", 0, 12)))
-    act(R("ss", 17, H, 2), pick(R("srow"), R("e0", 12, 12)), F.Copy)
+    turn_eo("l0t", "l0w")
     tt(tm(60, 18), tm(40, 18), jj(18), A.add)
-    ms(R("sst", 800, 16), BIG)
-    ts(REP[1], R("qi", 8, 18), 16.0, A.mult, 15.0, A.add)
-    ts(SPLO[1], tm(60, 18), 16.0, A.mult, 15.0, A.add)
-    turn("sst", 0, "ss", 0, C)
-    for i, r0 in enumerate((0.0, 1.0, 15.0)):
-        ts(SEL12[i], tm(2, 1), r0, A.add, 415.0, A.min)
-    cp(R("ssw"), pick(R("sst"), SELB))
-    act(R("spl", 0, 288), pick(R("ss", 16, C), SPLO[1]), F.Copy)
-    late[0]()
-    late[1]()
-    ts(SELE[1], tm(4, 2), 1.0, A.add, 831.0, A.min)
-    ts(K16, KC, 16.0, A.mult, 15.0, A.add)
+    ts(R("rkl", 24 - R1, 32), pick(R("l0t"), SELE[0]), 128.0, A.add)
+    send("e0", -1, R("own", R1, 48 - R1), R("rkl", 0, 48 - R1))
+    iota(R("iob"), [[1, PW]], 0, 0)
+    gfill(R("ww", H, C), 192)
+    gfill(R("ww", 576 + H, C), 192)
 
-    def zmake(t, win, stride, lst, tmp, vgaps, sgaps):
+    def zmake(t, win, stride, lst, tmp, vgaps, sgaps, qs):
         z, p = "z%d" % t, "p%d" % (t + 1)
         w = lambda b: R(win, stride * b, stride)
         act(tmp(0, 0, 96), pick(w(0), R(lst, 12, 6)), F.Copy)
@@ -395,27 +443,27 @@ def rank_program(g, core, T, topo):
         sgaps[0]()
         four("w", z, A4, H)
         vgaps[0]()
-        to_tile(p, A4, 0.03125)
+        to_tile(p, A4, 0.03125, qs)
+        sgaps[1]()
         quant(p, p)
         mm(0, "ur", 0, p, 0, H)
         mm(1, "ur", 0, p, 0, H)
         vgaps[1]()
-        sgaps[1]()
 
     def merge(t, win):
         o, hb, nb = OFS[t], C + H * (t - 1), (None, 24, 16)[t]
         row, bo, n1 = R("prow", H * (t - 1), H), R("lst", 12 * t, 12), 12 * nb
-        ends, extra = R("l1", 288 + nb - 1, 12, nb), R("sig1", 1, 16, S1)
-        own_scores(hb, 0, H)()
+        ends = R("l1", 288 + nb - 1, 12, nb)
+        own_scores(hb, 0, H, 0)()
         act(row, ps(1, H), F.Copy)
         for m in SROWS:
-            sign("sig1", S1, m, H, hb)
+            sign("sig1", S1, m, m, H, hb, 1)
         tt(R("l1", 0, n1), pick(R("hh", hb, H), REP[t]), R("spl", 288 * (t - 1), n1), A.is_ge)
         tt(R("eq", 0, H), ps(0, H), R("hh", hb, H), A.is_equal)
         scan(R("l1", 288, n1), R(("c24", "c16")[t - 1], 0, n1), R("l1", 0, n1), A.mult)
         scan(R("tie", 0, H), R("m2", 0, H), R("eq", 0, H), A.mult, A.subtract)
-        cp(bo, ends)
-        ts(R("tb", 0, 12), ends, 16.0, A.mult, -float(C), A.add)
+        ts(bo, ends, 16.0, A.mult, 15.0, A.add)
+        ts(R("tb", 0, 12), ends, 16.0, A.mult, float(H), A.add)
         tt(R("fb", 16, H), pick(R("ssw"), bo), row, A.is_le)
         vrow(VR[0], H, hb, -1.0)
         turn("ft", 0, "fb", 0, H)
@@ -423,74 +471,98 @@ def rank_program(g, core, T, topo):
         vsum(VR[0], H, 0.0)
         scan(R("fts"), R("c16"), R("ft"), A.mult)
         vrow(VR[0] + 1, H, hb, -1.0)
-        tt(extra, pick(R("fts"), SEL12[2]), R("tb", 16, 16), A.add)
+        tt(R("tb", 32, 16), pick(R("fts"), SEL12[2]), R("tb", 16, 16), A.add)
         for m in SROWS:
-            upper("sig1", S1, m, H, o)
+            lower("sig1", S1, m, m, o)
         for m in SROWS:
-            lower("sig1", S1, m, o)
+            upper("sig1", S1, m, m, H, o)
         for m in range(VR[0] + 1, VR[1]):
             if m + 1 < VR[1]:
                 vrow(m + 1, H, hb, -1.0)
+            else:
+                tt(R("tb", 48, 12), R("tb", 32, 12), R("a1", o, 12), A.subtract)
             vsum(m, H, 0.0)
-        nv = VR[1] - VR[0]
-        tt(R("a2", o + VR[0], nv), R("scv", 96 * VR[0] + 95, nv, 96), R("sig1", 1 + S1 * VR[0], nv, S1), A.add)
-        tt(R("rk", o, 12), R("a2", o, 12), R("a1", o, 12), A.subtract)
-        ts(R("rku", o, 12), R("rk", o, 12), float(C + H), A.add)
+        tt(R("tb", 64, 12), R("a2", o, 12), R("tb", 48, 12), A.add)
+        tt(R("rk", o, 12), R("sc1", 95, 12, 96), R("tb", 64, 12), A.add)
+        cp(R("rku", o, 12), R("rk", o, 12))
         if t == 2:
-            ts(OFF2, R("rk", o, 12), float(C + H), A.add, 192.0, A.min)
-            send("off2", prv, R("loff2"), OFF2)
+            ts(OFF2, R("rk", o, 12), 192.0, A.min)
+            send("off2", -1, R("loff2"), OFF2)
+            send("off3", 2, R("loff3"), OFF2)
         cp(pick(win, R("rku", o, 12)), R("mval"))
 
     def held_even(b):
-        act(R("heldp", 576 * b + H, H, 2), pick(R("tpu", C * b, C), R("le0", 0, 12)), F.Copy)
+        act(R("heldp", 576 * b + H, H, 2), pick(R("tpu", C * b, C), R("e0p", 0, 12)), F.Copy)
 
-    gfill(R("a2", OFS[1] + 11, 1), 0)
-    gfill(R("a2", OFS[2] + 11, 1), 0)
-    zmake(0, "tpu", C, "le0", lambda b, a, n: R("heldp", 576 * b + H + 1 + 2 * a, n, 2),
-          [lambda: (ts(tm(80, 32), jj(32), 192.0, A.is_ge, -383.0, A.mult), ts(tm(112, 32), jj(32), 2.0, A.mult, 192.0, A.add),
-                    ts(REP[2], R("i16", 0, 12), 15.0, A.add), ts(SPLO[2], R("i16", 0, 12), 0.0, A.mult, K16, A.add)),
-           lambda: (tt(R("s192", 0, 32), tm(80, 32), tm(112, 32), A.add), ts(SELN, tm(6, 2), 799.0, A.min))],
-          [lambda: (held_even(0), held_even(1)), lambda: None])
-    sendq("p", nxt, "p1", "lp")
+    def sorted_scores():
+        ts(SPLO[1], tm(60, 18), 16.0, A.mult, 15.0, A.add)
+        act(R("srow"), ps(1, C), F.Copy)
+        for o in range(2):
+            act(R("ss", o, H, 2), pick(R("srow"), R("e0", 12 * o, 12)), F.Copy)
+        act(R("spl", 0, 288), pick(R("ss"), SPLO[1]), F.Copy)
+
+    def merge_offsets():
+        ts(REP[1], R("qi", 8, 18), 16.0, A.mult, 15.0, A.add)
+        ms(R("ssw", C, 16), BIG)
+        ts(SEL12[2], tm(2, 1), 15.0, A.add, 415.0, A.min)
+        ts(tm(80, 32), jj(32), 192.0, A.is_ge, -383.0, A.mult)
+
+    zmake(0, "tpu", C, "e0p", lambda b, a, n: R("heldp", 576 * b + H + 1 + 2 * a, n, 2),
+          [merge_offsets, lambda: scan(R("ssw", 0, C), R("mbig"), R("ss"), A.max, A.min, init=-BIG)],
+          [sorted_scores, lambda: held_even(0)], "VVVV")
+    sendq("p", 1, "p1", "lp")
+    for a, n in ((0, 16), (400, 32), (816, 32), (1232, 32), (1648, 16)):
+        gfill(R("ar", a, n), 0)
+    gfill(R("o2row", H, 16), 192)
+    gfill(R("o3row", H, 16), 192)
+    gfill(R("pv", H, 12, PW), 0)
+    late = [unpack_own(0), unpack_own(1)]
     merge(1, R("win1"))
-    late = [unpack_own(2), unpack_own(3)]
     four("e", "lp", A4, H)
-    cp(R("hi", 0, 36), R("rku", 0, 36))
+    tt(R("s192", 0, 32), tm(80, 32), tm(112, 32), A.add)
     scan(R("mrow", 32, C), R("d0"), R("win1", 0, C), A.mult)
-    held_even(2)
-    held_even(3)
+    for b in range(1, 4):
+        held_even(b)
     for b in range(4):
         evac("S", R("heldp", 576 * b, H), A4[b], H, 0.5)
+    late[0]()
+    late[1]()
+    late = [unpack_own(2), unpack_own(3)]
+    cp(R("hi", 24, 12), R("rku", 24, 12))
     turn_eo("mtt", "mrow")
-    ts(R("hi", 48, 36), R("hi", 0, 36), 1, A.arith_shift_right)
+    cp(R("hi", 0, 24), RK0)
     tt(R("g1", 32, 32), pick(R("mtt"), SELE[0]), R("s192", 0, 32), A.add)
+    ts(SPLO[2], R("i16", 0, 12), 0.0, A.mult, K16, A.add)
     tt(R("g1", 64, 32), pick(R("mtt"), SELE[1]), R("g1", 32, 32), A.min)
+    ts(R("hi", 48, 36), R("hi", 0, 36), 1, A.arith_shift_right)
     cp(R("o1", 0, 24), R("g1", 64, 24))
-    send("o1", nxt, R("lo1"), R("o1", 0, 24))
+    send("o1", 1, R("lo1"), R("o1", 0, 24))
 
     late[0]()
     late[1]()
+    ts(REP[2], R("i16", 0, 12), 15.0, A.add)
     for o in range(2):
         cp(pick(R("ww", 0, 576), R("o1", 12 * o, 12)), R("iob", 0, H))
-    act(R("spl", 288, H), pick(R("ss", 16, C), SPLO[2]), F.Copy)
-    wrap_s(3, R("ww", H, C), RK0)
-    quant("v", "vb")
+    act(R("spl", 288, H), pick(R("ss"), SPLO[2]), F.Copy)
     late = []
     zmake(1, "heldp", 576, "lo1", lambda b, a, n: R("ztmp", H * b + a, n),
-          [lambda: late.append(wrap_v(3)),
-           lambda: (late[0](), ts(R("s192", 32, 16), jj(16), 192.0, A.add))],
-          [lambda: (sort_own(0), sort_own(1)), lambda: None])
+          [lambda: (quant("v", "vb"), ts(P1H, R("hi", 72, 12), 192.0, A.min), cp(A0H, R("hi", 48, 24))),
+           lambda: late.append(wrap_v(3))],
+          [lambda: (wrap_s(3, R("ww", H, C), RK0), sort_own(0)), lambda: sort_own(1)], "VVVV")
+    send("p1h", -1, R("lp1h"), P1H)
     four("e", "p2", A4, H)
     merge(2, R("win2"))
+    ts(SELN, tm(6, 2), 799.0, A.min)
     scan(R("mrow", 32, H), R("d0", 0, H), R("win2", 0, H), A.mult)
     for b in range(4):
         evac("S", R("heldo", HO * b, H), A4[b], H, 0.125)
     sort_own(2)
     sort_own(3)
-    ts(P1H, R("hi", 72, 12), 192.0, A.min)
+    ts(SEL12[0], tm(2, 1), 0.0, A.add, 415.0, A.min)
     turn("mtt", 0, "mrow", 16, H)
-    cp(A0H, R("hi", 48, 24))
+    ts(SEL12[1], tm(2, 1), 1.0, A.add, 415.0, A.min)
     tt(R("g1", 16, 16), pick(R("mtt", 0, 416), SEL12[0]), R("s192", 32, 16), A.add)
+    late[0]()
     tt(R("g1", 96, 16), pick(R("mtt", 0, 416), SEL12[1]), R("g1", 16, 16), A.min)
     cp(O2, R("g1", 96, 12))
     for b in (0, 2, 1, 3):
@@ -502,9 +574,9 @@ def rank_program(g, core, T, topo):
     quant("ee", "ee")
     four("w", "ee", A4, H)
     cp(pick(R("ww", 576, 576), O2), R("iob", 0, H))
-    to_tile("v2", A4, 0.03125, "SSVS")
+    to_tile("v2", A4, 0.03125, "SSVV")
     quant("v2", "v2")
-    sendq("v2", prv, "v2", "lb2")
+    sendq("v2", -1, "v2", "lb2")
 
     def leaves(out, i, prev, b, a, n):
         tt(out, pick(R("pv", PW * (4 * i + b), PW), R("xo", 32 * i + a // 16, n // 16)), R(prev, C * b + a, n), A.add)
@@ -519,34 +591,37 @@ def rank_program(g, core, T, topo):
     act(R("o2row", 0, H), pick(R("iob"), R("loff2")), F.Copy)
     planes(0, 2, 0.03125 / 8)
     planes(0, 3, 0.03125 / 8)
-    act(R("c1row"), pick(R("o2row"), P1H), F.Copy)
-    send("c1", prv, R("lc1"), R("c1row"))
     wrap_s(1, R("o2row"), R("xo", 96, 24))
+    act(R("o3row", 0, H), pick(R("iob"), R("loff3")), F.Copy)
+    act(R("c1row"), pick(R("o3row"), R("lp1h")), F.Copy)
     for b in range(4):
         leaves(R("x1", C * b, C), 0, "tu8", b, 0, C)
-    wrap_v(1)()
+    near = topo.chip(nxt) == topo.chip(core)
+    if not near:
+        wrap_s(2, R("c1row"), A0H)
+        late = wrap_v(1)
+        wrap_v(2)()
+        late()
     four("e", "lb2", A4, H)
     to_tile("b1", A4, 1.0, "SSSS")
     quant("b1", "b1")
-    sendq("b1", prv, "b1", "lb1")
+    sendq("b1", -1, "b1", "lb1")
 
     for b in range(4):
         planes(1, b, 0.25)
-    wrap_s(2, R("lc1"), A0H)
+    counts = [lambda: ts(R("cf", 0, 96), R("xo", 0, 96), 192.0, A.is_lt), lambda: tt(R("cf", 96, 24), R("cf", 0, 24), R("cf", 32, 24), A.add),
+              lambda: tt(R("cf", 128, 24), R("cf", 96, 24), R("cf", 64, 24), A.add), lambda: cp(CU, R("cf", 128, 24))]
+    if near:
+        wrap_s(2, R("c1row"), A0H)
+        wrap_v(1)()
+        counts = [lambda: wrap_v(2)(), lambda: (counts[4](), counts[5]()), lambda: counts[6](), lambda: counts[7]()] + counts
     for b in range(4):
         leaves(R("x2", C * b, C), 1, "x1", b, 0, C)
-        if b == 1:
-            late = wrap_v(2)
-        elif b == 2:
-            late()
-    ts(R("cf", 0, 96), R("xo", 0, 96), 192.0, A.is_lt)
-    tt(R("cf", 96, 24), R("cf", 0, 24), R("cf", 32, 24), A.add)
-    tt(R("cf", 128, 24), R("cf", 96, 24), R("cf", 64, 24), A.add)
-    cp(CU, R("cf", 128, 24))
+        counts[b]()
     four("e", "lb1", A4, H)
     for b in range(4):
         planes(2, b, 0.5)
-    act(R("ucr"), pick(R("ior", 0, 16), CU), F.Copy)
+    act(R("ucr"), pick(R("io16", 0, 16), CU), F.Copy)
     dma("Y", "out", T.uc[:], T.ucr[0:128:16, :], [R("ucr")], [])
     for hf, (a, n) in enumerate(((0, 256), (256, 128))):
         for b in range(4):
@@ -554,11 +629,10 @@ def rank_program(g, core, T, topo):
         quant("xx", "xx", a, n)
         mm(hf, "v", 0, "xx", a, n)
         dma("Y", "out", T.oc[:, 4 * a:4 * (a + n)], raw(R("q_xx", a, n)), [R("q_xx", a, n)], [])
-        if hf == 1:
-            for i in range(4):
-                dma("YS"[i % 2], "out", T.osc[4 * i:4 * i + 4, :], T.s_xx[32 * i:32 * i + 4, :], [R("s_xx")], [])
         act(R("yb", a, n), ps(hf, n), F.Copy)
         dma("S", "out", T.y[:, a:a + n], T.yb[:, a:a + n], [R("yb", a, n)], [])
+    for i in range(4):
+        dma("YYYS"[i], "out", T.osc[4 * i:4 * i + 4, :], T.s_xx[32 * i:32 * i + 4, :], [R("s_xx")], [])
     for s, n in cnt.items():
         if not any(seen[q].get(s, 0) >= n for q in Q):
             (g if s == "sent" else g.sync).wait_ge(T.sem[s], n)

import numpy as np
from concourse.mybir import dt, AluOpType as A, ActivationFunctionType as F

C, H = 384, 192
X4, U8, BF, F32, I32, U16 = "float8_e4m3fn_x4", "uint8", "bfloat16", "float32", "int32", "uint16"
CUT0 = (0, 8, 18, 21, 24)
R1 = CUT0[2]
VR = (3, 8)
PW = 208
S0, S1 = C + 2, H + 2
HO = 2 * H
BIG = 1.0e29

SCRATCH, PART = {}, {"ps": ("ps", 0, 4096)}


def _sb(dtype, **kw):
    for k, n in kw.items():
        SCRATCH[k] = ("sbuf", [128, n], dtype)
        PART[k] = (k, 0, n)


def _parts(buf, dtype, **kw):
    a = 0
    for k, n in kw.items():
        PART[k] = (buf, a, n)
        a += (n + 15) // 16 * 16
    SCRATCH[buf] = ("sbuf", [128, a], dtype)


_Q = dict(x=C, u=128, ur=128, v=128, w=512, e=512, lur=128, lx=C, z0=H, z1=H, p1=H, p2=H, lp=H, ee=H, v2=H, lb2=H, b1=H, lb1=H, xx=C)
for _k, _n in _Q.items():
    _sb(X4, **{"q_" + _k: _n})
    _sb(U8, **{"s_" + _k: _n})
_sb(BF, xb=4 * C, ub=512, vb=512, eb=516, ones=516,
    io16=256, m1=256, m2=256, mbig=C, c16=416, c24=288, iob=PW, iom=C, mval=H, d0=C, win1=576, win2=480, ww=2 * 576,
    tpu=4 * C, tu8=4 * C, heldp=4 * 576, heldo=4 * HO, ztmp=4 * H,
    z0=4 * H, z1=4 * H, p1=4 * H, p2=4 * H, ee=4 * H, v2=4 * H, b1=4 * H, xx=4 * C,
    pv=12 * PW, x1=4 * C, x2=4 * C,
    cmpv=24 * C, scv=24 * H, sc1=12 * 96, sig0=13 * S0, eq=C, tie=C, l1=576,
    fb=224, ft=416, fts=416, mrow=448, mtt=832, l0w=448, l0t=832, o2row=PW, o3row=PW, c1row=H,
    ar=416 * 4, att=800 * 4)
_parts("small", F32, cols=8, jj=32, i16=32, s192=48, tmp=160, a1=48, a2=48, tb=80, rk=48)
_sb(BF, ior=H)
_sb(F32, sig1=16 * S1, junk=8 * S0,
    srow=C, prow=2 * H, msk=C, hh=C + 2 * H,
    ss=C, ssw=C + 16, spl=288 + H, g1=128, cf=160, ucr=C, yb=C)
_sb(I32, pi=8, qi=32, hi=96)
_sb(U16, uo=8, ko=80, rku=48, own=48, rkp=R1, rkl=56 - R1, o1=32, lst=112, lo1=24, loff2=12, loff3=12, lp1h=12, xo=128)
PART["e0"], PART["e0p"] = ("own", 24, 24), ("rkl", 24 - R1, 24)
SCRATCH["ps"] = ("psum", [128, 4096], F32)

_DMA = ["x0", "x1", "u", "wc", "ws", "v", "out"]
_REM = ["qu", "su", "qx", "sx", "rk", "e0", "qp", "sp", "o1", "p1h", "off2", "off3", "qv2", "sv2", "qb1", "sb1"]
SEMAPHORES = ["cV", "cS", "cT", "cG", "sent", "sent0"] + ["d_" + k for k in _DMA] + ["r_" + k for k in _REM]


def R(name, a=0, n=None, step=1):
    buf, a0, width = PART[name]
    n = width - a if n is None else n
    return (buf, a0 + a, a0 + a + (n - 1) * step + 1, step, None)


def pick(win, offs):
    return win[:4] + (offs,)


def rank_program(g, core, T, topo):
    rank = T.rank_of(core)
    if rank is None:
        return
    N = len(T.cores)
    nxt = T.cores[(rank + 1) % N]
    Q = {"V": g.vector, "S": g.scalar, "T": g.tensor, "G": g, "Y": g.sync}
    cnt, seen, wr, rd = {}, {q: {} for q in Q}, {}, {}

    def ap(v):
        if not isinstance(v, tuple):
            return v
        a = T[v[0]][:, v[1]:v[2]:v[3]] if v[3] > 1 else T[v[0]][:, v[1]:v[2]]
        return a if v[4] is None else a.indirect(ap(v[4]))

    def cols(v):
        if v[0] == "ps":
            return slice(v[1] // 512 * 512, v[1] // 512 * 512 + 512)
        return slice(v[1], v[2], v[3])

    def views(l):
        l = [v for v in l if isinstance(v, tuple)]
        return l + [v[4] for v in l if v[4] is not None]

    def need(q, r, w):
        deps = {}
        for tab, vs in ((wr, r + w), (rd, w), (rd, [v for v in r if v[0] == "ps"])):
            for v in vs:
                for s, last in tab.get(v[0], {}).items():
                    if not (tab is rd and v[0] == "ps" and s == "c" + q):
                        deps[s] = max(deps.get(s, 0), int(last[cols(v)].max()))
        for s, n in deps.items():
            if seen[q].get(s, 0) < n:
                Q[q].wait_ge(T.sem[s], n)
                seen[q][s] = n

    def mark(s, n, r, w):
        for tab, vs in ((rd, r), (wr, w)):
            for v in vs:
                if tab is wr:
                    for t in (wr, rd):
                        for last in t.get(v[0], {}).values():
                            last[cols(v)] = 0
                tab.setdefault(v[0], {}).setdefault(s, np.zeros(SCRATCH[v[0]][1][1], np.int64))[cols(v)] = n

    def op(q, fn, r, w):
        r, w = views(r) + [v[4] for v in w if v[4] is not None], [v[:4] + (None,) for v in w]
        need(q, r, w)
        s = "c" + q
        cnt[s] = cnt.get(s, 0) + 1
        fn().then_inc(T.sem[s], 1)
        mark(s, cnt[s], r, w)

    def dma(q, name, out, in_, r, w):
        need(q, r, w)
        s = "d_" + name
        cnt[s] = cnt.get(s, 0) + 16
        Q[q].dma_start(out, in_).then_inc(T.sem[s], 16)
        if name != "out":
            mark(s, cnt[s], r, w)

    def raw(v):
        return ap(v).bitcast(dt.uint8) if SCRATCH[v[0]][2] == X4 else ap(v)

    def send(name, d, out, in_):
        dst, src = T.cores[(rank + d) % N], T.cores[(rank - d) % N]
        need("G", [in_], [])
        rid, pid, _ = topo.addr(dst)
        left = "sent0" if name in _REM[:5] else "sent"
        g.remote_dma(raw(out), raw(in_), T.sem["r_" + name], T.sem[left], pid, rid, topo.mask(core, dst))
        cnt[left] = cnt.get(left, 0) + len(topo.engines(core, dst))
        cnt["r_" + name] = len(topo.engines(src, core))
        mark("r_" + name, cnt["r_" + name], [], [out])

    def sendq(name, d, a, b):
        for k in "qs":
            send(k + name, d, R(k + "_" + b), R(k + "_" + a))

    V, S = g.vector, g.scalar
    fl = dict(allow_small_or_imprecise_dtypes=True)

    def ts(out, in0, s1, op0, s2=None, op1=None):
        more = () if op1 is None else (op1,)
        op("V", lambda: V.tensor_scalar(ap(out), ap(in0), ap(s1), ap(s2), op0, *more), [in0, s1, s2], [out])

    def tt(out, in0, in1, o):
        op("V", lambda: V.tensor_tensor(ap(out), ap(in0), ap(in1), o), [in0, in1], [out])

    def cp(out, in_):
        op("V", lambda: V.tensor_copy(ap(out), ap(in_)), [in_], [out])

    def ms(out, c):
        op("V", lambda: V.memset(ap(out), c), [], [out])

    def iota(out, pattern, base, mult):
        kw = {} if SCRATCH[out[0]][2] == I32 else fl
        op("G", lambda: g.iota(ap(out), pattern, base, mult, **kw), [], [out])

    def gfill(out, c, step=0):
        iota(out, [[step, len(range(out[1], out[2], out[3]))]], c, 0)

    def scan(out, d0, d1, o0, o1=A.add, init=0.0):
        op("V", lambda: V.tensor_tensor_scan(ap(out), ap(d0), ap(d1), ap(init), o0, o1), [d0, d1, init], [out])

    def tr(out, in_):
        op("V", lambda: V.transpose(ap(out), ap(in_)), [in_], [out])

    def act(out, in_, f, acc=None, **kw):
        more = {k: ap(v) for k, v in kw.items()}
        if acc is not None:
            more["accum_out"] = ap(acc)
        op("S", lambda: S.activation(ap(out), ap(in_), f, **more), [in_] + list(kw.values()), [out] + ([acc] if acc else []))

    def lin(out, in_, scale, bias):
        act(out, in_, F.Identity, scale=scale, bias=bias)

    def sfill(out, c):
        lin(out, R("ones", 0, len(range(out[1], out[2], out[3]))), 0.0, c)

    def quant(name, src, a=0, n=None, s0=None):
        n = _Q[name] if n is None else n
        qo, so, in_ = R("q_" + name, a, n), R("s_" + name, a, n), R(src, 4 * a if s0 is None else s0, 4 * n)
        op("V", lambda: V.quantize_mx(ap(qo), ap(so), ap(in_)), [in_], [qo, so])

    def pickq(name, src, offs):
        qo, qi = R("q_" + name), R("q_" + src)
        op("V", lambda: V.tensor_copy(ap(qo).bitcast(dt.uint32), ap(qi).bitcast(dt.uint32).indirect(ap(offs))), [qi, offs], [qo])
        act(R("s_" + name), pick(R("s_" + src), offs), F.Copy)

    def ps(bank, n, a=0):
        return R("ps", 512 * bank + a, n)

    def mm(bank, st, c0, mv, a, n):
        ins = [R("q_" + st, c0, 128), R("s_" + st, c0, 128), R("q_" + mv, a, n), R("s_" + mv, a, n)]
        op("T", lambda: g.tensor.matmul_mx(ap(ps(bank, n)), *[ap(v) for v in ins], True, True), ins, [ps(bank, n)])

    def four(st, mv, banks, n):
        for b in range(4):
            mm(banks[b], st, 128 * b, mv, 0, n)

    def evac(q, out, bank, n, scale):
        if q == "V":
            ts(out, ps(bank, n), scale, A.mult)
        else:
            act(out, ps(bank, n), F.Identity, scale=scale)

    def to_tile(name, banks, scale, qs):
        for b in range(4):
            evac(qs[b], R(name, b, H, 4), banks[b], H, scale)

    KC, ODD, P208, P400, ODD1, K1024, EVEN, K16 = [R("cols", i, 1) for i in range(8)]
    SELN, SELE = R("ko", 0, 2), (R("ko", 4, 2), R("ko", 6, 2))
    SEL12 = [R("ko", 8 + 2 * i, 1) for i in range(3)]
    REP, SPLO = (None, R("ko", 14, 18), R("ko", 50, 12)), (None, R("ko", 32, 18), R("ko", 62, 12))
    O2, P1H, A0H, CU, OFF2 = R("lst", 0, 12), R("lst", 36, 12), R("lst", 48, 24), R("lst", 72, 24), R("lst", 96, 12)
    RK0 = R("own", 0, 24)
    tm = lambda a, n: R("tmp", a, n)
    jj = lambda n: R("jj", 0, n)
    pi = lambda i, n=1: R("pi", i, n)
    A4, B2 = (2, 3, 4, 5), (6, 7)
    OFS = (0, 24, 36)
    SROWS = [m for m in range(12) if not VR[0] <= m < VR[1]]

    dma("S", "u", T.ub[:], T.u[:], [], [R("ub")])
    dma("Y", "x0", T.xb[:, 0:1024], T.x[:, 0:1024], [], [R("xb", 0, 1024)])
    dma("Y", "x1", T.xb[:, 1024:1536], T.x[:, 1024:1536], [], [R("xb", 1024, 512)])
    iota(pi(0), [[0, 1]], 0, 1)
    ms(R("ones"), 1.0)
    iota(R("i16"), [[16, 32]], 0, 0)
    iota(R("io16"), [[0, 16], [1, 16]], 0, 0)
    op("G", lambda: g.affine_select(ap(R("eb")), ap(R("ones")), [[-1, 516]], A.is_equal, 0.0, 3, 4), [R("ones")], [R("eb")])
    ms(R("c16"), 1.0)
    ts(pi(1), pi(0), 4, A.arith_shift_right)
    ts(pi(4), pi(0), 15, A.bitwise_and)
    ts(pi(5), pi(0), 1, A.bitwise_and)
    ms(R("c16", 0, 26, 16), 0.0)
    tt(pi(2), pi(0), pi(1), A.add)
    cp(R("cols", 0, 2), pi(4, 2))
    cp(R("uo", 0, 8), R("i16", 0, 8))
    ts(pi(3), pi(2), 1, A.bitwise_and)
    ts(jj(32), R("i16"), KC, A.add)
    scan(R("ior"), R("ones", 0, H), R("ones", 0, H), A.mult)
    ts(K1024, ODD, 1024.0, A.mult)
    ts(EVEN, ODD, -1.0, A.mult, 1.0, A.add)
    ts(P208, pi(3), 208.0, A.mult)
    ts(tm(0, 2), jj(2), 12.0, A.is_ge, 224.0, A.mult)
    ts(tm(2, 2), jj(2), 16.0, A.mult, P208, A.add)
    ts(R("m1"), R("io16"), KC, A.is_equal)
    tt(tm(4, 2), tm(0, 2), tm(2, 2), A.add)
    ts(R("m2"), R("io16"), KC, A.is_gt)
    ts(SELE[0], tm(4, 2), 831.0, A.min)
    for name, a, n in (("l0w", 0, 32), ("l0w", 416, 32), ("fb", 0, 16), ("fb", 208, 16), ("mrow", 0, 32), ("mrow", 416, 32)):
        sfill(R(name, a, n), 0.0)
    sfill(R("win1", 0, C), K1024)
    sfill(R("win2", 0, H), K1024)
    sfill(R("d0"), EVEN)
    quant("u", "ub")
    pickq("ur", "u", R("uo"))
    sendq("u", 1, "ur", "lur")
    quant("e", "eb", 0, 128, 3)
    quant("e", "eb", 128, 128, 2)
    ts(P400, pi(3), 400.0, A.mult)
    ts(SELE[1], tm(4, 2), 1.0, A.add, 831.0, A.min)
    quant("x", "xb", 0, 256)
    mm(2, "ur", 0, "x", 0, 256)
    quant("e", "eb", 256, 128, 1)
    quant("x", "xb", 256, 128)
    mm(1, "ur", 0, "x", 0, C)
    mm(0, "ur", 0, "x", 0, C)
    sendq("x", 1, "x", "lx")
    for a in (0, H):
        lin(R("mbig", a, H), R("m1", 0, H), 2 * BIG, -BIG)
    slot = 0
    for a, e in zip(CUT0[0::2], CUT0[1::2]):
        lin(R("sig0", S0 * slot, e - a, S0), R("i16", a, e - a), 1.0, 16.0 - C)
        slot += e - a
    lin(R("mval"), R("ior"), ODD, -1.0)
    lin(tm(16, 18), jj(18), 1.0 / 24.0, -11.5 / 24.0)
    lin(tm(6, 2), jj(2), 16.0, P400)
    lin(K16, KC, 16.0, 15.0)
    lin(tm(112, 32), jj(32), 2.0, 192.0)
    lin(R("s192", 32, 16), jj(16), 1.0, 192.0)
    iota(R("iom"), [[1, C]], -128, 0)

    def own_scores(hb, a, n, bank):
        tt(R("msk", a, n), ps(bank, n, a), R("m1", 0, n), A.mult)
        return lambda: scan(R("hh", hb + a, n), R("c16", a, n), R("msk", a, n), A.mult)

    def sign(sig, st, i, m, n, hb, bank):
        act(R(sig, st * i + 2, n), ps(bank, n), F.Sign, scale=-1.0, bias=R("hh", hb + 16 * m + 15, 1))

    def lower(sig, st, i, m, o):
        e = 16 * (m + 1)
        act(R("junk", S0 * (i % 4), e + 2), R(sig, st * i, e + 2), F.Relu, acc=R("a1", o + m, 1), scale=-1.0)

    def upper(sig, st, i, m, n, o):
        e = 16 * (m + 1)
        if e < n:
            act(R("junk", S0 * (4 + i % 4), n - e), R(sig, st * i + 2 + e, n - e), F.Relu, acc=R("a2", o + m, 1))

    def vrow(m, n, hb, off, bank=0):
        e, own = 16 * (m + 1), R("hh", hb + 16 * m + 15, 1)
        ts(R("cmpv", n * m, e), ps(bank, e), own, A.is_le, off, A.add)
        if e < n:
            ts(R("cmpv", n * m + e, n - e), ps(bank, n - e, e), own, A.is_lt, off, A.add)

    def vsum(m, n, init):
        h = n // 2
        scan(R("scv" if n == C else "sc1", h * m, h), R("cmpv", n * m, h), R("cmpv", n * m + h, h), A.add, init=init)

    def turn_eo(dst, src):
        for o in (0, 1):
            tr(R(dst, 416 * o, H), R(src, 32 + o, H, 2))
            tr(R(dst, 416 * o + H, 224), R(src, o, 224, 2))

    def turn(dst, d0, src, s0, n):
        tr(R(dst, d0, n), R(src, s0 + 16, n))
        tr(R(dst, d0 + n, n + 32), R(src, s0, n + 32))

    def wrap_s(i, win, offs):
        act(R("ar", 416 * i + 16, C), pick(win, offs), F.Copy)

    def wrap_v(i):
        turn("att", 800 * i, "ar", 416 * i, C)
        return lambda: cp(R("xo", 32 * i, 32), pick(R("att", 800 * i, 800), SELN))

    def sort_own(b):
        for o in range(2):
            act(R("heldo", HO * b + H + o, 96, 2), pick(R("tu8", C * b, C), R("e0", 12 * o, 6)), F.Copy)

    def unpack_own(b):
        mm(B2[b % 2], "e", 128 * b, "x", 0, C)
        return lambda: evac("S", R("tu8", C * b, C), B2[b % 2], C, 0.125)

    def ties(bank, a, n):
        tt(R("eq", a, n), ps(bank, n, a), R("hh", a, n), A.is_equal)
        return lambda: scan(R("tie", a, n), R("m2", 0, n), R("eq", a, n), A.mult, A.subtract)

    def srows(rows, slot, bank):
        for i in range(len(rows) + 2):
            if 0 < i + 1 < len(rows):
                sign("sig0", S0, slot + i + 1, rows[i + 1], C, 0, bank)
            if i < len(rows):
                upper("sig0", S0, slot + i, rows[i], C, 0)
            if i >= 2:
                lower("sig0", S0, slot + i - 2, rows[i - 2], 0)

    def vrows(rows, bank, after={}):
        for i, m in enumerate(rows):
            if i + 2 < len(rows):
                vrow(rows[i + 2], C, 0, -0.5, bank)
            vsum(m, C, R("tie", 16 * m + 15, 1))
            if m in after:
                after[m]()

    def splaces(out, rows, fill):
        tt(R("rk", rows[0], len(rows)), R("a2", rows[0], len(rows)), R("a1", rows[0], len(rows)), A.subtract)
        fill()
        ts(out, R("rk", rows[0], len(rows)), float(C), A.add)

    def vplaces(out, rows):
        ts(out, R("scv", H * rows[0] + H - 1, len(rows), H), C / 2, A.add)

    sa, va, sb, vb = [list(range(a, e)) for a, e in zip(CUT0[:-1], CUT0[1:])]
    eh = 16 * R1
    first = own_scores(0, 0, 16 * len(sa), 2)
    rest = own_scores(0, 16 * len(sa), 256 - 16 * len(sa), 2)
    first()
    rest()
    sign("sig0", S0, 0, 0, C, 0, 1)
    late = ties(2, 0, 256)
    quant("e", "eb", 384, 128, 0)
    late()
    late = own_scores(0, 256, eh - 256, 0) if eh > 256 else lambda: None
    cp(R("sig0", 1, len(sa), S0), R("tie", 15, len(sa), 16))
    late()
    vrow(va[0], C, 0, -0.5, 0)
    late = ties(0, 256, eh - 256) if eh > 256 else lambda: None
    vrow(va[1], C, 0, -0.5, 0)
    late()
    srows(sa, 0, 1)
    mm(6, "lur", 0, "lx", 0, C)
    mm(7, "lur", 0, "lx", 0, C)
    late = []
    vrows(va, 0, {va[-3]: lambda: late.append(own_scores(0, eh, C - eh, 6)), va[-2]: lambda: late[0]()})
    splaces(R("own", 0, len(sa)), sa, lambda: vplaces(R("own", va[0], len(va)), va))
    send("rk", 1, R("rkp", 0, R1), R("own", 0, R1))
    g.sync.wait_ge(T.sem.sent0, cnt["sent0"])
    seen["Y"]["sent0"] = cnt["sent0"]
    dma("Y", "wc", raw(R("q_w")), T.wc[:], [], [R("q_w")])
    dma("Y", "ws", T.s_w[:], T.ws[:], [], [R("s_w")])
    dma("Y", "v", T.vb[:], T.v[:], [], [R("vb")])
    four("e", "lx", A4, C)
    slot = len(sa)
    sign("sig0", S0, slot, sb[0], C, 0, 7)
    late = ties(6, eh, C - eh)
    vrow(vb[0], C, 0, -0.5, 6)
    late()
    vrow(vb[1], C, 0, -0.5, 6)
    cp(R("sig0", 1 + S0 * slot, len(sb), S0), R("tie", 16 * sb[0] + 15, len(sb), 16))
    srows(sb, slot, 7)
    vrows(vb, 6)
    gfill(R("c24"), 1)
    gfill(R("c24", 0, 12, 24), 0)
    gfill(R("sig1", 0, 12, S1), 16 - H, 16)
    gfill(R("sig1", 1, 12, S1), 0)
    gfill(R("a1", 24, 24), 0)
    gfill(R("a2", 24, 24), 0)
    gfill(R("sc1", 95, 12, 96), 0)
    gfill(R("tb", 16, 16), 0)
    cp(pick(R("l0w", 32, C), R("rkp", 0, R1)), R("iom", 0, eh))
    splaces(R("rkl", 0, len(sb)), sb, lambda: vplaces(R("rkl", len(sb), len(vb)), vb))
    for b in range(4):
        evac("S", R("tpu", C * b, C), A4[b], C, 0.5)
    cp(R("qi", 8, 18), tm(16, 18))
    cp(pick(R("l0w", 32, C), R("rkl", 0, 24 - R1)), R("iom", eh, C - eh))
    ts(tm(40, 18), R("qi", 8, 18), -24.0, A.mult)
    turn_eo("l0t", "l0w")
    tt(tm(60, 18), tm(40, 18), jj(18), A.add)
    ts(R("rkl", 24 - R1, 32), pick(R("l0t"), SELE[0]), 128.0, A.add)
    send("e0", -1, R("own", R1, 48 - R1), R("rkl", 0, 48 - R1))
    iota(R("iob"), [[1, PW]], 0, 0)
    gfill(R("ww", H, C), 192)
    gfill(R("ww", 576 + H, C), 192)

    def zmake(t, win, stride, lst, tmp, vgaps, sgaps, qs):
        z, p = "z%d" % t, "p%d" % (t + 1)
        w = lambda b: R(win, stride * b, stride)
        act(tmp(0, 0, 96), pick(w(0), R(lst, 12, 6)), F.Copy)
        cp(tmp(0, 96, 96), pick(w(0), R(lst, 18, 6)))
        for b in range(4):
            if b > 0:
                act(tmp(b, 0, H), pick(w(b), R(lst, 12, 12)), F.Copy)
            tt(R(z, b, H, 4), pick(w(b), R(lst, 0, 12)), tmp(b, 0, H), A.add)
        quant(z, z)
        sgaps[0]()
        four("w", z, A4, H)
        vgaps[0]()
        to_tile(p, A4, 0.03125, qs)
        sgaps[1]()
        quant(p, p)
        mm(0, "ur", 0, p, 0, H)
        mm(1, "ur", 0, p, 0, H)
        vgaps[1]()

    def merge(t, win):
        o, hb, nb = OFS[t], C + H * (t - 1), (None, 24, 16)[t]
        row, bo, n1 = R("prow", H * (t - 1), H), R("lst", 12 * t, 12), 12 * nb
        ends = R("l1", 288 + nb - 1, 12, nb)
        own_scores(hb, 0, H, 0)()
        act(row, ps(1, H), F.Copy)
        for m in SROWS:
            sign("sig1", S1, m, m, H, hb, 1)
        tt(R("l1", 0, n1), pick(R("hh", hb, H), REP[t]), R("spl", 288 * (t - 1), n1), A.is_ge)
        tt(R("eq", 0, H), ps(0, H), R("hh", hb, H), A.is_equal)
        scan(R("l1", 288, n1), R(("c24", "c16")[t - 1], 0, n1), R("l1", 0, n1), A.mult)
        scan(R("tie", 0, H), R("m2", 0, H), R("eq", 0, H), A.mult, A.subtract)
        ts(bo, ends, 16.0, A.mult, 15.0, A.add)
        ts(R("tb", 0, 12), ends, 16.0, A.mult, float(H), A.add)
        tt(R("fb", 16, H), pick(R("ssw"), bo), row, A.is_le)
        vrow(VR[0], H, hb, -1.0)
        turn("ft", 0, "fb", 0, H)
        tt(R("tb", 16, 12), R("tb", 0, 12), R("tie", 15, 12, 16), A.add)
        vsum(VR[0], H, 0.0)
        scan(R("fts"), R("c16"), R("ft"), A.mult)
        vrow(VR[0] + 1, H, hb, -1.0)
        tt(R("tb", 32, 16), pick(R("fts"), SEL12[2]), R("tb", 16, 16), A.add)
        for m in SROWS:
            lower("sig1", S1, m, m, o)
        for m in SROWS:
            upper("sig1", S1, m, m, H, o)
        for m in range(VR[0] + 1, VR[1]):
            if m + 1 < VR[1]:
                vrow(m + 1, H, hb, -1.0)
            else:
                tt(R("tb", 48, 12), R("tb", 32, 12), R("a1", o, 12), A.subtract)
            vsum(m, H, 0.0)
        tt(R("tb", 64, 12), R("a2", o, 12), R("tb", 48, 12), A.add)
        tt(R("rk", o, 12), R("sc1", 95, 12, 96), R("tb", 64, 12), A.add)
        cp(R("rku", o, 12), R("rk", o, 12))
        if t == 2:
            ts(OFF2, R("rk", o, 12), 192.0, A.min)
            send("off2", -1, R("loff2"), OFF2)
            send("off3", 2, R("loff3"), OFF2)
        cp(pick(win, R("rku", o, 12)), R("mval"))

    def held_even(b):
        act(R("heldp", 576 * b + H, H, 2), pick(R("tpu", C * b, C), R("e0p", 0, 12)), F.Copy)

    def sorted_scores():
        ts(SPLO[1], tm(60, 18), 16.0, A.mult, 15.0, A.add)
        act(R("srow"), ps(1, C), F.Copy)
        for o in range(2):
            act(R("ss", o, H, 2), pick(R("srow"), R("e0", 12 * o, 12)), F.Copy)
        act(R("spl", 0, 288), pick(R("ss"), SPLO[1]), F.Copy)

    def merge_offsets():
        ts(REP[1], R("qi", 8, 18), 16.0, A.mult, 15.0, A.add)
        ms(R("ssw", C, 16), BIG)
        ts(SEL12[2], tm(2, 1), 15.0, A.add, 415.0, A.min)
        ts(tm(80, 32), jj(32), 192.0, A.is_ge, -383.0, A.mult)

    zmake(0, "tpu", C, "e0p", lambda b, a, n: R("heldp", 576 * b + H + 1 + 2 * a, n, 2),
          [merge_offsets, lambda: scan(R("ssw", 0, C), R("mbig"), R("ss"), A.max, A.min, init=-BIG)],
          [sorted_scores, lambda: held_even(0)], "VVVV")
    sendq("p", 1, "p1", "lp")
    for a, n in ((0, 16), (400, 32), (816, 32), (1232, 32), (1648, 16)):
        gfill(R("ar", a, n), 0)
    gfill(R("o2row", H, 16), 192)
    gfill(R("o3row", H, 16), 192)
    gfill(R("pv", H, 12, PW), 0)
    late = [unpack_own(0), unpack_own(1)]
    merge(1, R("win1"))
    four("e", "lp", A4, H)
    tt(R("s192", 0, 32), tm(80, 32), tm(112, 32), A.add)
    scan(R("mrow", 32, C), R("d0"), R("win1", 0, C), A.mult)
    for b in range(1, 4):
        held_even(b)
    for b in range(4):
        evac("S", R("heldp", 576 * b, H), A4[b], H, 0.5)
    late[0]()
    late[1]()
    late = [unpack_own(2), unpack_own(3)]
    cp(R("hi", 24, 12), R("rku", 24, 12))
    turn_eo("mtt", "mrow")
    cp(R("hi", 0, 24), RK0)
    tt(R("g1", 32, 32), pick(R("mtt"), SELE[0]), R("s192", 0, 32), A.add)
    ts(SPLO[2], R("i16", 0, 12), 0.0, A.mult, K16, A.add)
    tt(R("g1", 64, 32), pick(R("mtt"), SELE[1]), R("g1", 32, 32), A.min)
    ts(R("hi", 48, 36), R("hi", 0, 36), 1, A.arith_shift_right)
    cp(R("o1", 0, 24), R("g1", 64, 24))
    send("o1", 1, R("lo1"), R("o1", 0, 24))

    late[0]()
    late[1]()
    ts(REP[2], R("i16", 0, 12), 15.0, A.add)
    for o in range(2):
        cp(pick(R("ww", 0, 576), R("o1", 12 * o, 12)), R("iob", 0, H))
    act(R("spl", 288, H), pick(R("ss"), SPLO[2]), F.Copy)
    late = []
    zmake(1, "heldp", 576, "lo1", lambda b, a, n: R("ztmp", H * b + a, n),
          [lambda: (quant("v", "vb"), ts(P1H, R("hi", 72, 12), 192.0, A.min), cp(A0H, R("hi", 48, 24))),
           lambda: late.append(wrap_v(3))],
          [lambda: (wrap_s(3, R("ww", H, C), RK0), sort_own(0)), lambda: sort_own(1)], "VVVV")
    send("p1h", -1, R("lp1h"), P1H)
    four("e", "p2", A4, H)
    merge(2, R("win2"))
    ts(SELN, tm(6, 2), 799.0, A.min)
    scan(R("mrow", 32, H), R("d0", 0, H), R("win2", 0, H), A.mult)
    for b in range(4):
        evac("S", R("heldo", HO * b, H), A4[b], H, 0.125)
    sort_own(2)
    sort_own(3)
    ts(SEL12[0], tm(2, 1), 0.0, A.add, 415.0, A.min)
    turn("mtt", 0, "mrow", 16, H)
    ts(SEL12[1], tm(2, 1), 1.0, A.add, 415.0, A.min)
    tt(R("g1", 16, 16), pick(R("mtt", 0, 416), SEL12[0]), R("s192", 32, 16), A.add)
    late[0]()
    tt(R("g1", 96, 16), pick(R("mtt", 0, 416), SEL12[1]), R("g1", 16, 16), A.min)
    cp(O2, R("g1", 96, 12))
    for b in (0, 2, 1, 3):
        w = pick(R("heldo", HO * b, HO), O2)
        if b < 2:
            ts(R("ee", b, H, 4), w, 8.0, A.mult)
        else:
            act(R("ee", b, H, 4), w, F.Identity, scale=8.0)
    quant("ee", "ee")
    four("w", "ee", A4, H)
    cp(pick(R("ww", 576, 576), O2), R("iob", 0, H))
    to_tile("v2", A4, 0.03125, "SSVV")
    quant("v2", "v2")
    sendq("v2", -1, "v2", "lb2")

    def leaves(out, i, prev, b, a, n):
        tt(out, pick(R("pv", PW * (4 * i + b), PW), R("xo", 32 * i + a // 16, n // 16)), R(prev, C * b + a, n), A.add)

    def planes(i, b, scale):
        evac("S", R("pv", PW * (4 * i + b), H), A4[b], H, scale)

    wrap_s(0, R("ww", 576 + H, C), RK0)
    planes(0, 0, 0.03125 / 8)
    wrap_v(0)()
    planes(0, 1, 0.03125 / 8)
    act(R("o2row", 0, H), pick(R("iob"), R("loff2")), F.Copy)
    planes(0, 2, 0.03125 / 8)
    planes(0, 3, 0.03125 / 8)
    wrap_s(1, R("o2row"), R("xo", 96, 24))
    act(R("o3row", 0, H), pick(R("iob"), R("loff3")), F.Copy)
    act(R("c1row"), pick(R("o3row"), R("lp1h")), F.Copy)
    for b in range(4):
        leaves(R("x1", C * b, C), 0, "tu8", b, 0, C)
    near = topo.chip(nxt) == topo.chip(core)
    if not near:
        wrap_s(2, R("c1row"), A0H)
        late = wrap_v(1)
        wrap_v(2)()
        late()
    four("e", "lb2", A4, H)
    to_tile("b1", A4, 1.0, "SSSS")
    quant("b1", "b1")
    sendq("b1", -1, "b1", "lb1")

    for b in range(4):
        planes(1, b, 0.25)
    counts = [lambda: ts(R("cf", 0, 96), R("xo", 0, 96), 192.0, A.is_lt), lambda: tt(R("cf", 96, 24), R("cf", 0, 24), R("cf", 32, 24), A.add),
              lambda: tt(R("cf", 128, 24), R("cf", 96, 24), R("cf", 64, 24), A.add), lambda: cp(CU, R("cf", 128, 24))]
    if near:
        wrap_s(2, R("c1row"), A0H)
        wrap_v(1)()
        counts = [lambda: wrap_v(2)(), lambda: (counts[4](), counts[5]()), lambda: counts[6](), lambda: counts[7]()] + counts
    for b in range(4):
        leaves(R("x2", C * b, C), 1, "x1", b, 0, C)
        counts[b]()
    four("e", "lb1", A4, H)
    for b in range(4):
        planes(2, b, 0.5)
    act(R("ucr"), pick(R("io16", 0, 16), CU), F.Copy)
    dma("Y", "out", T.uc[:], T.ucr[0:128:16, :], [R("ucr")], [])
    for hf, (a, n) in enumerate(((0, 256), (256, 128))):
        for b in range(4):
            leaves(R("xx", 4 * a + b, n, 4), 2, "x2", b, a, n)
        quant("xx", "xx", a, n)
        mm(hf, "v", 0, "xx", a, n)
        dma("Y", "out", T.oc[:, 4 * a:4 * (a + n)], raw(R("q_xx", a, n)), [R("q_xx", a, n)], [])
        act(R("yb", a, n), ps(hf, n), F.Copy)
        dma("S", "out", T.y[:, a:a + n], T.yb[:, a:a + n], [R("yb", a, n)], [])
    for i in range(4):
        dma("YYYS"[i], "out", T.osc[4 * i:4 * i + 4, :], T.s_xx[32 * i:32 * i + 4, :], [R("s_xx")], [])
    for s, n in cnt.items():
        if not any(seen[q].get(s, 0) >= n for q in Q):
            (g if s == "sent" else g.sync).wait_ge(T.sem[s], n)
